import numpy as np
import ml_dtypes


def mxq(x, axis, fmt="e4m3"):
    dtype, down = {"e4m3": (ml_dtypes.float8_e4m3fn, 7), "e5m2": (ml_dtypes.float8_e5m2, 14)}[fmt]
    v = np.moveaxis(np.asarray(x, np.float32).astype(ml_dtypes.bfloat16).astype(np.float64), axis, -1)
    blocks = v.reshape(v.shape[:-1] + (-1, 32))
    amax = np.abs(blocks).max(-1, keepdims=True)
    byte = np.maximum(np.where(amax > 0, np.frexp(amax)[1] - 1 + 127, 0) - down, 1)
    scale = np.exp2(byte - 127.0)
    codes = (blocks / scale).astype(np.float32).astype(dtype).astype(np.float64)
    return np.moveaxis((codes * scale).reshape(v.shape), -1, axis)


WIDE = False


def mx_kscale(k):
    if not WIDE:
        return np.ones(k)
    levels = np.array([10, -10, 5, -5, 0])
    if k % 512:
        return np.exp2(np.random.permutation(np.resize(levels, k // 32))).repeat(32)
    a = np.empty((k // 512, 16))
    for p in range(k // 512):
        a[p, :8] = np.random.permutation(np.resize(levels, 8))
        for g in range(8):
            far = levels[np.abs(levels - a[p, g]) >= 10]
            a[p, g + 8] = far[np.random.randint(len(far))]
    return np.exp2(a.ravel()).repeat(32)


def f64(x):
    return np.asarray(x).astype(np.float64)


def striped(idx):
    return np.tile(idx.reshape(-1, 16).T, (8, 1)).astype(np.uint16)


def unstriped(offs):
    return offs[:16].T.reshape(-1).astype(np.int64)


E2M1 = np.array([0.0, 0.5, 1.0, 1.5, 2.0, 3.0, 4.0, 6.0, -0.0, -0.5, -1.0, -1.5, -2.0, -3.0, -4.0, -6.0])


def pack_weight(w, fmt):
    k, n = w.shape
    w = f64(np.asarray(w, np.float32).astype(ml_dtypes.bfloat16)).reshape(k // 32, 32, n)
    amax = np.abs(w).max(1)
    if fmt == "e4m3":
        byte = np.frexp(amax)[1] - 1 + 127 - 7
    else:
        mant, ex = np.frexp(amax / 6.0)
        byte = np.where(mant > 0.5, ex, ex - 1) + 127
    byte = np.clip(np.where(amax > 0, byte, 1), 1, 254)
    scaled = (w * np.exp2(127.0 - byte)[:, None, :]).reshape(k, n).astype(np.float32)
    by_word = np.ascontiguousarray(scaled.reshape(k // 512, 128, 4, n).transpose(0, 1, 3, 2))
    if fmt == "e4m3":
        words = by_word.astype(ml_dtypes.float8_e4m3fn).view(np.uint8)
    else:
        c = by_word.astype(ml_dtypes.float4_e2m1fn).view(np.uint8) & 0xF
        words = (c[..., 0::2] | (c[..., 1::2] << 4)).reshape(k // 512, 128, 2 * n)
    return np.ascontiguousarray(words), np.ascontiguousarray(byte.astype(np.uint8).reshape(k // 512, 16, n))


def unpack_weight(words, scales, fmt):
    g, _, n = scales.shape
    words = np.ascontiguousarray(words).reshape(g, 128, n, -1)
    if fmt == "e4m3":
        vals = words.view(ml_dtypes.float8_e4m3fn).astype(np.float64)
    else:
        nib = np.empty((g, 128, n, 4), np.uint8)
        nib[..., 0::2] = words & 0xF
        nib[..., 1::2] = words >> 4
        vals = E2M1[nib]
    vals = vals * np.repeat(np.exp2(scales.astype(np.float64) - 127.0), 8, axis=1)[..., None]
    return vals.transpose(0, 1, 3, 2).reshape(g * 512, n)


def gelu(v):
    return 0.5 * v * (1.0 + np.tanh(np.sqrt(2.0 / np.pi) * (v + 0.044715 * v**3)))


K, H, N, T, S, T2, R = 512, 1536, 512, 2048, 1024, 2048, 128

def setup_inputs():
    n = np.random.standard_normal
    s = mx_kscale(K)[:, None]
    u = mx_kscale(H)[:, None]
    tab_words, tab_scales = pack_weight(n((K, T)) * s, "e4m3")
    wg_words, wg_scales = pack_weight(n((K, H)) / np.sqrt(K) / s, "e2m1")
    wu = (n((K, H)) / np.sqrt(K) / s * u.T).astype(np.float32)
    wd_words, wd_scales = pack_weight(2.0 * n((H, N)) / np.sqrt(H) / u, "e4m3")
    wgo = np.exp(0.3 * n((R, S))).astype(np.float32)
    offs = striped(np.random.permutation(T)[:S])
    offs2 = striped(np.random.permutation(T2)[:S])
    return {"tab_words": tab_words, "tab_scales": tab_scales,
            "wg_words": wg_words, "wg_scales": wg_scales, "wu": wu,
            "wd_words": wd_words, "wd_scales": wd_scales,
            "wgo": wgo, "offs": offs, "offs2": offs2}

def reference(tab_words, tab_scales, wg_words, wg_scales, wu, wd_words, wd_scales, wgo, offs, offs2):
    v = unpack_weight(tab_words, tab_scales, "e4m3")[:, unstriped(offs)]
    wg = unpack_weight(wg_words, wg_scales, "e2m1")
    wd = unpack_weight(wd_words, wd_scales, "e4m3")
    a = wg.T @ v
    b = mxq(f64(wu), 0, "e4m3").T @ v
    h = a / (1.0 + np.exp(-a)) * b
    y = wd.T @ mxq(h, 0, "e4m3")
    out = np.zeros((N, T2))
    out[:, unstriped(offs2)] = np.tile(f64(wgo), (N // R, 1)) * y
    return out

@@ -1,0 +1,234 @@
+from contextlib import ExitStack
+
+import concourse.mybir as mybir
+
+K, H, N, T, S, T2 = 512, 1536, 512, 2048, 1024, 2048
+FLOPS = 2 * S * (2 * K * H + H * N)
+
+F32 = mybir.dt.float32
+BF16 = mybir.dt.bfloat16
+I32 = mybir.dt.int32
+U32 = mybir.dt.uint32
+U16 = mybir.dt.uint16
+U8 = mybir.dt.uint8
+FP8X4 = mybir.dt.float8_e4m3fn_x4
+FP4X4 = mybir.dt.float4_e2m1fn_x4
+MULT = mybir.AluOpType.mult
+SILU = mybir.ActivationFunctionType.Silu
+
+P = 128
+PACK = 4
+PASS = P * PACK
+BLOCKS = H // PASS
+HALF = 512
+CHUNK = 128
+PIECE = 256
+LIST_ROWS = 16
+WINDOWS = 2
+
+
+def tile_list_accepted_swiglu_cache_kernel(
+    tc, tab_words, tab_scales, wg_words, wg_scales, wu, wd_words, wd_scales, wgo, offs, offs2, out
+):
+    nc = tc.nc
+    with ExitStack() as ctx:
+        keep = ctx.enter_context(tc.tile_pool(name="keep", bufs=1))
+        ring = ctx.enter_context(tc.tile_pool(name="ring", bufs=2))
+        psum = ctx.enter_context(tc.psum_pool(name="psum", bufs=1))
+
+        pick = keep.tile([P, S // LIST_ROWS], U16, name="pick")
+        place = keep.tile([P, S // LIST_ROWS], U16, name="place")
+        tab_w = keep.tile([P, T], I32, name="tab_w", align_bytes=64)
+        tab_s = keep.tile([P, T // 4], I32, name="tab_s", align_bytes=64)
+        wg_w = keep.tile([P, 2 * H], U8, name="wg_w", align_bytes=64)
+        wg_s = keep.tile([P, H], U8, name="wg_s", align_bytes=64)
+        wu_bf = [keep.tile([P, PASS * PACK], BF16, name="wu_bf%d" % g, align_bytes=64) for g in range(BLOCKS)]
+        wu_w = keep.tile([P, H], U32, name="wu_w", align_bytes=64)
+        wu_s = keep.tile([P, H], U8, name="wu_s", align_bytes=64)
+        v_w = keep.tile([P, S], U32, name="v_w", align_bytes=64)
+        v_s = keep.tile([P, S], U8, name="v_s", align_bytes=64)
+        h_w = keep.tile([P, BLOCKS, S], U32, name="h_w", align_bytes=64)
+        h_s = keep.tile([P, BLOCKS, S], U8, name="h_s", align_bytes=64)
+        windows = [keep.tile([P, T2], F32, name="window%d" % i, align_bytes=64) for i in range(WINDOWS)]
+
+        warm = keep.tile([P, 8], F32, name="warm", tag="slot_a", align_bytes=64)
+        wg_w_raw = keep.tile([P, 2 * H // 4], I32, name="wg_w_raw", tag="slot_b", align_bytes=64)
+        wg_s_raw = keep.tile([P, H // 4], I32, name="wg_s_raw", tag="slot_c", align_bytes=64)
+
+        nc.vector.memset(tab_s[:], 0)
+        nc.vector.memset(warm[:, 0:4], 0.0)
+        nc.vector.memset(wg_s_raw[:], 0)
+        nc.scalar.activation(warm[:, 4:8], warm[:, 0:4], SILU)
+
+        wu_raw = {}
+
+        def load_wu(g, tag):
+            wu_raw[g] = keep.tile([P, PACK, PASS], F32, name="wu_raw%d" % g, tag=tag, align_bytes=64)
+            nc.sync.dma_start(wu_raw[g][:], wu[:, g * PASS : (g + 1) * PASS].rearrange("(p j) c -> p j c", j=PACK))
+
+        nc.sync.dma_start(pick[:], offs)
+        nc.sync.dma_start(tab_w[:], tab_words[0].rearrange("p t i -> p (t i)").bitcast(I32))
+        load_wu(0, "slot_d")
+        for q in range(4):
+            nc.scalar.dma_start(tab_s[32 * q : 32 * q + 4, :], tab_scales[0, 4 * q : 4 * q + 4, :].bitcast(I32))
+        nc.sync.dma_start(wg_w_raw[:], wg_words[0].bitcast(I32))
+        for q in range(4):
+            nc.scalar.dma_start(wg_s_raw[32 * q : 32 * q + 4, :], wg_scales[0, 4 * q : 4 * q + 4, :].bitcast(I32))
+        load_wu(1, "slot_a")
+        nc.sync.dma_start(place[:], offs2)
+
+        for w in windows:
+            nc.vector.memset(w[:], 0.0)
+
+        def permute_wg_words(g):
+            cols = slice(g * PASS, (g + 1) * PASS)
+            nc.vector.tensor_copy(
+                wg_w[:].bitcast(U16)[:, cols].rearrange("p (t m) -> p t m", t=PACK),
+                wg_w_raw[:].bitcast(U16)[:, cols].rearrange("p (m t) -> p t m", t=PACK),
+            )
+
+        def permute_wg_scales(g):
+            cols = slice(g * PASS, (g + 1) * PASS)
+            nc.vector.tensor_copy(
+                wg_s[:, cols].rearrange("p (t m) -> p t m", t=PACK),
+                wg_s_raw[:].bitcast(U8)[:, cols].rearrange("p (m t) -> p t m", t=PACK),
+            )
+
+        def gather(piece):
+            cols = slice(piece * PIECE, (piece + 1) * PIECE)
+            entries = pick[:, piece * PIECE // LIST_ROWS : (piece + 1) * PIECE // LIST_ROWS]
+            nc.vector.tensor_copy(v_w[:, cols], tab_w[:].bitcast(U32).indirect(entries))
+            nc.vector.tensor_copy(v_s[:, cols], tab_s[:].bitcast(U8).indirect(entries))
+
+        def cast_wu(g, part, parts):
+            ms = slice(part * P // parts, (part + 1) * P // parts)
+            nc.scalar.copy(
+                wu_bf[g][:].rearrange("p (t m j) -> p m t j", t=PACK, j=PACK)[:, ms],
+                wu_raw[g][:].rearrange("p j (m t) -> p m t j", t=PACK)[:, ms],
+            )
+
+        def quantize_wu(g):
+            cols = slice(g * PASS, (g + 1) * PASS)
+            nc.vector.quantize_mx(out=wu_w[:, cols].bitcast(FP8X4), scales=wu_s[:, cols], in_=wu_bf[g][:])
+
+        def gate(g, chunk):
+            tokens = slice(chunk * CHUNK, (chunk + 1) * CHUNK)
+            a_ps = psum.tile([P, PACK, CHUNK], F32, name="a_ps", tag="a_ps", bufs=3)
+            for t in range(PACK):
+                c0 = g * PASS + t * P
+                nc.tensor.matmul_mx(
+                    out=a_ps[:, t, :],
+                    lhsT=wg_w[:, 2 * c0 : 2 * (c0 + P)].bitcast(FP4X4),
+                    lhsT_scale=wg_s[:, c0 : c0 + P],
+                    rhs=v_w[:, tokens].bitcast(FP8X4),
+                    rhs_scale=v_s[:, tokens],
+                    start=True,
+                    stop=True,
+                )
+            act = ring.tile([P, CHUNK, PACK], F32, name="act", tag="act", bufs=8, align_bytes=64)
+            nc.scalar.activation(act[:], a_ps[:].rearrange("p t n -> p n t"), SILU)
+            return act
+
+        def up_times_gate(g, chunk, act, h_bf):
+            tokens = slice(chunk * CHUNK, (chunk + 1) * CHUNK)
+            b_ps = psum.tile([P, PACK, CHUNK], F32, name="b_ps", tag="b_ps", bufs=3)
+            for t in range(PACK):
+                c0 = g * PASS + t * P
+                nc.tensor.matmul_mx(
+                    out=b_ps[:, t, :],
+                    lhsT=wu_w[:, c0 : c0 + P].bitcast(FP8X4),
+                    lhsT_scale=wu_s[:, c0 : c0 + P],
+                    rhs=v_w[:, tokens].bitcast(FP8X4),
+                    rhs_scale=v_s[:, tokens],
+                    start=True,
+                    stop=True,
+                )
+            c = chunk % (HALF // CHUNK)
+            nc.vector.tensor_tensor(
+                h_bf[:, c * CHUNK : (c + 1) * CHUNK, :], b_ps[:].rearrange("p t n -> p n t"), act[:], MULT
+            )
+
+        def quantize_h(g, half, h_bf):
+            tokens = slice(half * HALF, (half + 1) * HALF)
+            nc.vector.quantize_mx(
+                out=h_w[:, g, tokens].bitcast(FP8X4),
+                scales=h_s[:, g, tokens],
+                in_=h_bf[:].rearrange("p n t -> p (n t)"),
+            )
+
+        def down(nb, half):
+            tokens = slice(half * HALF, (half + 1) * HALF)
+            rows = slice(nb * P, (nb + 1) * P)
+            y_ps = psum.tile([P, HALF], F32, name="y_ps", tag="y_ps", bufs=2)
+            for g in range(BLOCKS):
+                nc.tensor.matmul_mx(
+                    out=y_ps[:],
+                    lhsT=wd_w[:, g, rows].bitcast(FP8X4),
+                    lhsT_scale=wd_s[:].bitcast(U8)[:, g, rows],
+                    rhs=h_w[:, g, tokens].bitcast(FP8X4),
+                    rhs_scale=h_s[:, g, tokens],
+                    start=(g == 0),
+                    stop=(g == BLOCKS - 1),
+                )
+            y_sb = ring.tile([P, HALF], F32, name="y_sb", tag="y_sb", bufs=8, align_bytes=64)
+            nc.vector.tensor_tensor(y_sb[:], y_ps[:], wgo_t[:, tokens], MULT)
+            return y_sb
+
+        def scatter(nb, half, y_sb):
+            entries = place[:, half * HALF // LIST_ROWS : (half + 1) * HALF // LIST_ROWS]
+            nc.vector.tensor_copy(windows[nb % WINDOWS][:].indirect(entries), y_sb[:])
+
+        gather(0)
+        for g in range(BLOCKS):
+            permute_wg_words(g)
+        load_wu(2, "slot_b")
+        permute_wg_scales(0)
+        cast_wu(0, 0, 1)
+        wd_w = keep.tile([P, BLOCKS, N], I32, name="wd_w", tag="slot_d", align_bytes=64)
+        nc.sync.dma_start(wd_w[:], wd_words.rearrange("a p n i -> p a (n i)").bitcast(I32))
+        quantize_wu(0)
+        for piece in range(1, S // PIECE):
+            gather(piece)
+        permute_wg_scales(1)
+        permute_wg_scales(2)
+        wd_s = keep.tile([P, BLOCKS, N // 4], I32, name="wd_s", tag="slot_c", align_bytes=64)
+        nc.gpsimd.memset(wd_s[:], 0)
+        for q in range(4):
+            nc.sync.dma_start(
+                wd_s[32 * q : 32 * q + 4, :, :],
+                wd_scales[:, 4 * q : 4 * q + 4, :].rearrange("a r n -> r a n").bitcast(I32),
+            )
+
+        pending = None
+        y_tiles = {}
+        for g in range(BLOCKS):
+            for half in range(S // HALF):
+                h_bf = ring.tile([P, HALF, PACK], BF16, name="h_bf", tag="h_bf", bufs=3, align_bytes=64)
+                for c in range(HALF // CHUNK):
+                    chunk = half * (HALF // CHUNK) + c
+                    act = gate(g, chunk)
+                    if g + 1 < BLOCKS and chunk % 2 == 1 and chunk < 7:
+                        cast_wu(g + 1, chunk // 2, 4)
+                    if g + 1 < BLOCKS and chunk == 6:
+                        cast_wu(g + 1, 3, 4)
+                    up_times_gate(g, chunk, act, h_bf)
+                    if c == 0 and pending is not None:
+                        quantize_h(*pending)
+                    if g + 1 < BLOCKS and chunk == 6:
+                        quantize_wu(g + 1)
+                    if g == 0 and chunk == 6:
+                        wgo_t = keep.tile([P, S], F32, name="wgo_t", tag="slot_a", align_bytes=64)
+                        nc.sync.dma_start(wgo_t[:], wgo)
+                    if g == BLOCKS - 1 and half == 1 and c >= 2:
+                        y_tiles[c - 2, 0] = down(c - 2, 0)
+                pending = (g, half, h_bf)
+        quantize_h(*pending)
+        for nb in range(2, N // P):
+            y_tiles[nb, 0] = down(nb, 0)
+        for nb in range(N // P):
+            y_tiles[nb, 1] = down(nb, 1)
+
+        for nb in range(N // P):
+            for half in range(S // HALF):
+                scatter(nb, half, y_tiles[nb, half])
+            nc.sync.dma_start(out[nb * P : (nb + 1) * P, :], windows[nb % WINDOWS][:])

@@ -22,9 +22,12 @@ PASS = P * PACK
 BLOCKS = H // PASS
 HALF = 512
 CHUNK = 128
-PIECE = 256
+PIECE = 512
 LIST_ROWS = 16
-WINDOWS = 2
+WINDOWS = 3
+GROUPS = ((0, 512), (512, 512))
+VECTOR_UNITS = (range(12), range(12))
+LAST_GPSIMD_UNIT = (None, 4, 8)
 
 
 def tile_list_accepted_swiglu_cache_kernel(
@@ -42,77 +45,83 @@ def tile_list_accepted_swiglu_cache_kernel(
         tab_s = keep.tile([P, T // 4], I32, name="tab_s", align_bytes=64)
         wg_w = keep.tile([P, 2 * H], U8, name="wg_w", align_bytes=64)
         wg_s = keep.tile([P, H], U8, name="wg_s", align_bytes=64)
-        wu_bf = [keep.tile([P, PASS * PACK], BF16, name="wu_bf%d" % g, align_bytes=64) for g in range(BLOCKS)]
+        wu_bf = [
+            keep.tile([P, PASS * PACK], BF16, name="wu_bf%d" % g, tag="wu_bf%d" % g, align_bytes=64)
+            for g in range(BLOCKS)
+        ]
         wu_w = keep.tile([P, H], U32, name="wu_w", align_bytes=64)
         wu_s = keep.tile([P, H], U8, name="wu_s", align_bytes=64)
-        v_w = keep.tile([P, S], U32, name="v_w", align_bytes=64)
-        v_s = keep.tile([P, S], U8, name="v_s", align_bytes=64)
-        h_w = keep.tile([P, BLOCKS, S], U32, name="h_w", align_bytes=64)
-        h_s = keep.tile([P, BLOCKS, S], U8, name="h_s", align_bytes=64)
-        windows = [keep.tile([P, T2], F32, name="window%d" % i, align_bytes=64) for i in range(WINDOWS)]
+        v_w = {}
+        v_s = {}
+        h_w = [keep.tile([P, BLOCKS * n], U32, name="h_w%d" % i, align_bytes=64) for i, (s0, n) in enumerate(GROUPS)]
+        h_s = [keep.tile([P, BLOCKS * n], U8, name="h_s%d" % i, align_bytes=64) for i, (s0, n) in enumerate(GROUPS)]
+        windows = [keep.tile([P, T2], F32, name="window%d" % i, align_bytes=64) for i in range(WINDOWS - 1)]
 
-        warm = keep.tile([P, 8], F32, name="warm", tag="slot_a", align_bytes=64)
+        warm_in = keep.tile([P, 4], F32, name="warm_in", tag="slot_a", align_bytes=64)
+        warm_out = keep.tile([P, 4], F32, name="warm_out", align_bytes=64)
         wg_w_raw = keep.tile([P, 2 * H // 4], I32, name="wg_w_raw", tag="slot_b", align_bytes=64)
-        wg_s_raw = keep.tile([P, H // 4], I32, name="wg_s_raw", tag="slot_c", align_bytes=64)
+        wg_s_raw = keep.tile([P, H // 4], I32, name="wg_s_raw", tag="slot_d", align_bytes=64)
 
         nc.vector.memset(tab_s[:], 0)
-        nc.vector.memset(warm[:, 0:4], 0.0)
+        nc.vector.memset(warm_in[:], 0.0)
+        nc.scalar.activation(warm_out[:], warm_in[:], SILU)
+        nc.vector.memset(windows[0][:], 0.0)
+        nc.vector.memset(windows[1][:], 0.0)
         nc.vector.memset(wg_s_raw[:], 0)
-        nc.scalar.activation(warm[:, 4:8], warm[:, 0:4], SILU)
 
-        wu_raw = {}
+        wu_first = keep.tile([P, PACK, PASS], F32, name="wu_first", tag="slot_a", align_bytes=64)
+        wu_raw = {0: wu_first[:]}
 
-        def load_wu(g, tag):
-            wu_raw[g] = keep.tile([P, PACK, PASS], F32, name="wu_raw%d" % g, tag=tag, align_bytes=64)
-            nc.sync.dma_start(wu_raw[g][:], wu[:, g * PASS : (g + 1) * PASS].rearrange("(p j) c -> p j c", j=PACK))
+        def load_wu(g):
+            nc.sync.dma_start(wu_raw[g], wu[:, g * PASS : (g + 1) * PASS].rearrange("(p j) c -> p j c", j=PACK))
 
+        nc.sync.dma_start(wg_w_raw[:], wg_words[0].bitcast(I32))
         nc.sync.dma_start(pick[:], offs)
         nc.sync.dma_start(tab_w[:], tab_words[0].rearrange("p t i -> p (t i)").bitcast(I32))
-        load_wu(0, "slot_d")
         for q in range(4):
-            nc.scalar.dma_start(tab_s[32 * q : 32 * q + 4, :], tab_scales[0, 4 * q : 4 * q + 4, :].bitcast(I32))
-        nc.sync.dma_start(wg_w_raw[:], wg_words[0].bitcast(I32))
+            nc.sync.dma_start(tab_s[32 * q : 32 * q + 4, :], tab_scales[0, 4 * q : 4 * q + 4, :].bitcast(I32))
+        load_wu(0)
         for q in range(4):
-            nc.scalar.dma_start(wg_s_raw[32 * q : 32 * q + 4, :], wg_scales[0, 4 * q : 4 * q + 4, :].bitcast(I32))
-        load_wu(1, "slot_a")
+            nc.sync.dma_start(wg_s_raw[32 * q : 32 * q + 4, :], wg_scales[0, 4 * q : 4 * q + 4, :].bitcast(I32))
         nc.sync.dma_start(place[:], offs2)
-
-        for w in windows:
-            nc.vector.memset(w[:], 0.0)
 
         def permute_wg_words(g):
             cols = slice(g * PASS, (g + 1) * PASS)
             nc.vector.tensor_copy(
-                wg_w[:].bitcast(U16)[:, cols].rearrange("p (t m) -> p t m", t=PACK),
-                wg_w_raw[:].bitcast(U16)[:, cols].rearrange("p (m t) -> p t m", t=PACK),
+                wg_w[:].bitcast(U16)[:, cols].rearrange("p (t b i) -> p b t i", t=PACK, i=8),
+                wg_w_raw[:].bitcast(U16)[:, cols].rearrange("p (b i t) -> p b t i", t=PACK, i=8),
             )
 
         def permute_wg_scales(g):
             cols = slice(g * PASS, (g + 1) * PASS)
             nc.vector.tensor_copy(
-                wg_s[:, cols].rearrange("p (t m) -> p t m", t=PACK),
-                wg_s_raw[:].bitcast(U8)[:, cols].rearrange("p (m t) -> p t m", t=PACK),
+                wg_s[:, cols].rearrange("p (t b i) -> p b t i", t=PACK, i=16),
+                wg_s_raw[:].bitcast(U8)[:, cols].rearrange("p (b i t) -> p b t i", t=PACK, i=16),
             )
 
-        def gather(piece):
-            cols = slice(piece * PIECE, (piece + 1) * PIECE)
+        def gather_words(piece, tag):
+            v_w[piece] = keep.tile([P, PIECE], U32, name="v_w%d" % piece, tag=tag, align_bytes=64)
             entries = pick[:, piece * PIECE // LIST_ROWS : (piece + 1) * PIECE // LIST_ROWS]
-            nc.vector.tensor_copy(v_w[:, cols], tab_w[:].bitcast(U32).indirect(entries))
-            nc.vector.tensor_copy(v_s[:, cols], tab_s[:].bitcast(U8).indirect(entries))
+            nc.vector.tensor_copy(v_w[piece][:], tab_w[:].bitcast(U32).indirect(entries))
 
-        def cast_wu(g, part, parts):
-            ms = slice(part * P // parts, (part + 1) * P // parts)
-            nc.scalar.copy(
+        def gather_scales(piece, tag):
+            v_s[piece] = keep.tile([P, PIECE], U8, name="v_s%d" % piece, tag=tag, align_bytes=64)
+            entries = pick[:, piece * PIECE // LIST_ROWS : (piece + 1) * PIECE // LIST_ROWS]
+            nc.vector.tensor_copy(v_s[piece][:], tab_s[:].bitcast(U8).indirect(entries))
+
+        def cast_wu(g, copy_op, ms=slice(0, P)):
+            copy_op(
                 wu_bf[g][:].rearrange("p (t m j) -> p m t j", t=PACK, j=PACK)[:, ms],
-                wu_raw[g][:].rearrange("p j (m t) -> p m t j", t=PACK)[:, ms],
+                wu_raw[g].rearrange("p j (m t) -> p m t j", t=PACK)[:, ms],
             )
 
         def quantize_wu(g):
             cols = slice(g * PASS, (g + 1) * PASS)
             nc.vector.quantize_mx(out=wu_w[:, cols].bitcast(FP8X4), scales=wu_s[:, cols], in_=wu_bf[g][:])
 
-        def gate(g, chunk):
-            tokens = slice(chunk * CHUNK, (chunk + 1) * CHUNK)
+        def gate(g, chunk, last):
+            piece, c0 = divmod(chunk * CHUNK, PIECE)
+            tokens = slice(c0, c0 + CHUNK)
             a_ps = psum.tile([P, PACK, CHUNK], F32, name="a_ps", tag="a_ps", bufs=3)
             for t in range(PACK):
                 c0 = g * PASS + t * P
@@ -120,17 +129,20 @@ def tile_list_accepted_swiglu_cache_kernel(
                     out=a_ps[:, t, :],
                     lhsT=wg_w[:, 2 * c0 : 2 * (c0 + P)].bitcast(FP4X4),
                     lhsT_scale=wg_s[:, c0 : c0 + P],
-                    rhs=v_w[:, tokens].bitcast(FP8X4),
-                    rhs_scale=v_s[:, tokens],
+                    rhs=v_w[piece][:, tokens].bitcast(FP8X4),
+                    rhs_scale=v_s[piece][:, tokens],
                     start=True,
                     stop=True,
                 )
-            act = ring.tile([P, CHUNK, PACK], F32, name="act", tag="act", bufs=8, align_bytes=64)
+            act = ring.tile(
+                [P, CHUNK, PACK], F32, name="act", tag="held" if last else "act", bufs=1 if last else 8, align_bytes=64
+            )
             nc.scalar.activation(act[:], a_ps[:].rearrange("p t n -> p n t"), SILU)
             return act
 
-        def up_times_gate(g, chunk, act, h_bf):
-            tokens = slice(chunk * CHUNK, (chunk + 1) * CHUNK)
+        def up_times_gate(g, chunk, act, h_out, on_vector, last):
+            piece, c0 = divmod(chunk * CHUNK, PIECE)
+            tokens = slice(c0, c0 + CHUNK)
             b_ps = psum.tile([P, PACK, CHUNK], F32, name="b_ps", tag="b_ps", bufs=3)
             for t in range(PACK):
                 c0 = g * PASS + t * P
@@ -138,97 +150,130 @@ def tile_list_accepted_swiglu_cache_kernel(
                     out=b_ps[:, t, :],
                     lhsT=wu_w[:, c0 : c0 + P].bitcast(FP8X4),
                     lhsT_scale=wu_s[:, c0 : c0 + P],
-                    rhs=v_w[:, tokens].bitcast(FP8X4),
-                    rhs_scale=v_s[:, tokens],
+                    rhs=v_w[piece][:, tokens].bitcast(FP8X4),
+                    rhs_scale=v_s[piece][:, tokens],
                     start=True,
                     stop=True,
                 )
-            c = chunk % (HALF // CHUNK)
-            nc.vector.tensor_tensor(
-                h_bf[:, c * CHUNK : (c + 1) * CHUNK, :], b_ps[:].rearrange("p t n -> p n t"), act[:], MULT
-            )
+            if on_vector:
+                nc.vector.tensor_tensor(h_out, b_ps[:].rearrange("p t n -> p n t"), act[:], MULT)
+            else:
+                b_sb = ring.tile(
+                    [P, CHUNK, PACK], F32, name="b_sb", tag="held" if last else "b_sb", bufs=1 if last else 8, align_bytes=64
+                )
+                nc.scalar.copy(b_sb[:], b_ps[:].rearrange("p t n -> p n t"))
+                nc.gpsimd.tensor_tensor(
+                    h_out.rearrange("p n t -> p (n t)"),
+                    b_sb[:].rearrange("p n t -> p (n t)"),
+                    act[:].rearrange("p n t -> p (n t)"),
+                    MULT,
+                )
 
-        def quantize_h(g, half, h_bf):
-            tokens = slice(half * HALF, (half + 1) * HALF)
-            nc.vector.quantize_mx(
-                out=h_w[:, g, tokens].bitcast(FP8X4),
-                scales=h_s[:, g, tokens],
-                in_=h_bf[:].rearrange("p n t -> p (n t)"),
-            )
+        def unit(i, u, h_bf):
+            s0, n = GROUPS[i]
+            g, c = divmod(u, n // CHUNK)
+            chunk = s0 // CHUNK + c
+            act = gate(g, chunk, (i, u) == (1, 10))
+            up_times_gate(g, chunk, act, h_bf[:, g, c * CHUNK : (c + 1) * CHUNK, :], u in VECTOR_UNITS[i], u == LAST_GPSIMD_UNIT[i])
 
-        def down(nb, half):
-            tokens = slice(half * HALF, (half + 1) * HALF)
+        def quantize_h(i, h_bf, g):
+            s0, n = GROUPS[i]
+            flat = h_bf[:].rearrange("p g n t -> p (g n t)")
+            for w0, w1 in ((g * n, (g + 1) * n),):
+                nc.vector.quantize_mx(
+                    out=h_w[i][:, w0:w1].bitcast(FP8X4), scales=h_s[i][:, w0:w1], in_=flat[:, PACK * w0 : PACK * w1]
+                )
+
+        def down(i, nb):
+            s0, n = GROUPS[i]
             rows = slice(nb * P, (nb + 1) * P)
-            y_ps = psum.tile([P, HALF], F32, name="y_ps", tag="y_ps", bufs=2)
+            y_ps = psum.tile([P, n], F32, name="y_ps", tag="y_ps", bufs=2)
             for g in range(BLOCKS):
                 nc.tensor.matmul_mx(
                     out=y_ps[:],
                     lhsT=wd_w[:, g, rows].bitcast(FP8X4),
                     lhsT_scale=wd_s[:].bitcast(U8)[:, g, rows],
-                    rhs=h_w[:, g, tokens].bitcast(FP8X4),
-                    rhs_scale=h_s[:, g, tokens],
+                    rhs=h_w[i][:, g * n : (g + 1) * n].bitcast(FP8X4),
+                    rhs_scale=h_s[i][:, g * n : (g + 1) * n],
                     start=(g == 0),
                     stop=(g == BLOCKS - 1),
                 )
-            y_sb = ring.tile([P, HALF], F32, name="y_sb", tag="y_sb", bufs=8, align_bytes=64)
-            nc.vector.tensor_tensor(y_sb[:], y_ps[:], wgo_t[:, tokens], MULT)
-            return y_sb
+            y_banks[i, nb] = y_ps
 
-        def scatter(nb, half, y_sb):
-            entries = place[:, half * HALF // LIST_ROWS : (half + 1) * HALF // LIST_ROWS]
-            nc.vector.tensor_copy(windows[nb % WINDOWS][:].indirect(entries), y_sb[:])
+        def weigh(i, nb):
+            s0, n = GROUPS[i]
+            if (i, nb) == (0, 0):
+                y_held = ring.tile([P, n], F32, name="y_held", tag="held", bufs=1, align_bytes=64)
+                y_tiles[i, nb] = y_held[:]
+            else:
+                y_tiles[i, nb] = y_sb[nb][:, s0 : s0 + n]
+            nc.scalar.copy(y_tiles[i, nb], y_banks[i, nb][:])
 
-        gather(0)
+        def scatter(nb, s0, n, values):
+            window = windows[nb % 2]
+            target = window[:].indirect(place[:, s0 // LIST_ROWS : (s0 + n) // LIST_ROWS])
+            nc.vector.tensor_tensor(target, values, wgo_t[:, s0 : s0 + n], MULT)
+            if s0 + n == S:
+                nc.sync.dma_start(out[nb * P : (nb + 1) * P, :], window[:])
+
+        y_sb = [keep.tile([P, S], F32, name="y_sb%d" % nb, align_bytes=64) for nb in range(4)]
+        y_tiles = {}
+        y_banks = {}
+        def h_tile(i):
+            return keep.tile([P, BLOCKS, GROUPS[i][1], PACK], BF16, name="h_bf%d" % i, align_bytes=64)
+
+        gather_words(0, "v_w0")
+        gather_scales(0, "v_s0")
         for g in range(BLOCKS):
             permute_wg_words(g)
-        load_wu(2, "slot_b")
+        wu_rest = keep.tile([P, BLOCKS - 1, PACK, PASS], F32, name="wu_rest", tag="slot_b", align_bytes=64)
+        for g in (1, 2):
+            wu_raw[g] = wu_rest[:, g - 1]
+            load_wu(g)
         permute_wg_scales(0)
-        cast_wu(0, 0, 1)
-        wd_w = keep.tile([P, BLOCKS, N], I32, name="wd_w", tag="slot_d", align_bytes=64)
-        nc.sync.dma_start(wd_w[:], wd_words.rearrange("a p n i -> p a (n i)").bitcast(I32))
+        cast_wu(0, nc.scalar.copy)
         quantize_wu(0)
-        for piece in range(1, S // PIECE):
-            gather(piece)
+        wd_w = keep.tile([P, BLOCKS, N], I32, name="wd_w", tag="slot_a", align_bytes=64)
+        nc.sync.dma_start(wd_w[:], wd_words.rearrange("a p n i -> p a (n i)").bitcast(I32))
         permute_wg_scales(1)
         permute_wg_scales(2)
-        wd_s = keep.tile([P, BLOCKS, N // 4], I32, name="wd_s", tag="slot_c", align_bytes=64)
-        nc.gpsimd.memset(wd_s[:], 0)
+        wd_s = keep.tile([P, BLOCKS, N // 4], I32, name="wd_s", tag="slot_d", align_bytes=64)
+        nc.vector.memset(wd_s[:], 0)
         for q in range(4):
             nc.sync.dma_start(
                 wd_s[32 * q : 32 * q + 4, :, :],
                 wd_scales[:, 4 * q : 4 * q + 4, :].rearrange("a r n -> r a n").bitcast(I32),
             )
-
+        gather_words(1, "v_w1")
+        gather_scales(1, "wu_bf0")
+        h_bf = [h_tile(0), h_tile(1)]
         pending = None
-        y_tiles = {}
         for g in range(BLOCKS):
-            for half in range(S // HALF):
-                h_bf = ring.tile([P, HALF, PACK], BF16, name="h_bf", tag="h_bf", bufs=3, align_bytes=64)
-                for c in range(HALF // CHUNK):
-                    chunk = half * (HALF // CHUNK) + c
-                    act = gate(g, chunk)
-                    if g + 1 < BLOCKS and chunk % 2 == 1 and chunk < 7:
-                        cast_wu(g + 1, chunk // 2, 4)
-                    if g + 1 < BLOCKS and chunk == 6:
-                        cast_wu(g + 1, 3, 4)
-                    up_times_gate(g, chunk, act, h_bf)
+            for i in range(2):
+                for c in range(4):
+                    unit(i, 4 * g + c, h_bf[i])
+                    step = 4 * i + c
+                    if g + 1 < BLOCKS and step in (1, 3, 5, 6):
+                        part = (1, 3, 5, 6).index(step)
+                        cast_wu(g + 1, nc.scalar.copy, slice(32 * part, 32 * part + 32))
                     if c == 0 and pending is not None:
                         quantize_h(*pending)
-                    if g + 1 < BLOCKS and chunk == 6:
+                    if g + 1 < BLOCKS and step == 6:
                         quantize_wu(g + 1)
-                    if g == 0 and chunk == 6:
-                        wgo_t = keep.tile([P, S], F32, name="wgo_t", tag="slot_a", align_bytes=64)
+                    if g == 1 and step == 6:
+                        wgo_t = keep.tile([P, S], F32, name="wgo_t", tag="slot_b", align_bytes=64)
                         nc.sync.dma_start(wgo_t[:], wgo)
-                    if g == BLOCKS - 1 and half == 1 and c >= 2:
-                        y_tiles[c - 2, 0] = down(c - 2, 0)
-                pending = (g, half, h_bf)
+                    if g == 2 and i == 1:
+                        down(0, c)
+                        if c > 0:
+                            weigh(0, c)
+                pending = (i, h_bf[i], g)
         quantize_h(*pending)
-        for nb in range(2, N // P):
-            y_tiles[nb, 0] = down(nb, 0)
-        for nb in range(N // P):
-            y_tiles[nb, 1] = down(nb, 1)
-
-        for nb in range(N // P):
-            for half in range(S // HALF):
-                scatter(nb, half, y_tiles[nb, half])
-            nc.sync.dma_start(out[nb * P : (nb + 1) * P, :], windows[nb % WINDOWS][:])
+        weigh(0, 0)
+        scatter(0, 0, 512, y_tiles[0, 0])
+        for nb in range(4):
+            down(1, nb)
+            weigh(1, nb)
+        scatter(0, 512, 512, y_tiles[1, 0])
+        for nb in range(1, 4):
+            scatter(nb, 0, S, y_sb[nb][:])

@@ -111,8 +111,8 @@ def tile_list_accepted_swiglu_cache_kernel(
 
         def cast_wu(g, copy_op, ms=slice(0, P)):
             copy_op(
-                wu_bf[g][:].rearrange("p (t m j) -> p m t j", t=PACK, j=PACK)[:, ms],
-                wu_raw[g].rearrange("p j (m t) -> p m t j", t=PACK)[:, ms],
+                wu_bf[g][:].rearrange("p (t m j) -> p m j t", t=PACK, j=PACK)[:, ms],
+                wu_raw[g].rearrange("p j (m t) -> p m j t", t=PACK)[:, ms],
             )
 
         def quantize_wu(g):
@@ -173,7 +173,7 @@ def tile_list_accepted_swiglu_cache_kernel(
             s0, n = GROUPS[i]
             g, c = divmod(u, n // CHUNK)
             chunk = s0 // CHUNK + c
-            act = gate(g, chunk, (i, u) == (1, 10))
+            act = gate(g, chunk, (i, u) == (1, 11))
             up_times_gate(g, chunk, act, h_bf[:, g, c * CHUNK : (c + 1) * CHUNK, :], u in VECTOR_UNITS[i], u == LAST_GPSIMD_UNIT[i])
 
         def quantize_h(i, h_bf, g):
@@ -200,21 +200,20 @@ def tile_list_accepted_swiglu_cache_kernel(
                 )
             y_banks[i, nb] = y_ps
 
-        def weigh(i, nb):
+        def evacuate(i, nb):
             s0, n = GROUPS[i]
-            if (i, nb) == (0, 0):
-                y_held = ring.tile([P, n], F32, name="y_held", tag="held", bufs=1, align_bytes=64)
-                y_tiles[i, nb] = y_held[:]
-            else:
-                y_tiles[i, nb] = y_sb[nb][:, s0 : s0 + n]
-            nc.scalar.copy(y_tiles[i, nb], y_banks[i, nb][:])
+            nc.scalar.copy(y_sb[nb][:, s0 : s0 + n], y_banks[i, nb][:])
 
         def scatter(nb, s0, n, values):
             window = windows[nb % 2]
-            target = window[:].indirect(place[:, s0 // LIST_ROWS : (s0 + n) // LIST_ROWS])
-            nc.vector.tensor_tensor(target, values, wgo_t[:, s0 : s0 + n], MULT)
+            nc.vector.tensor_copy(window[:].indirect(place[:, s0 // LIST_ROWS : (s0 + n) // LIST_ROWS]), values)
             if s0 + n == S:
                 nc.sync.dma_start(out[nb * P : (nb + 1) * P, :], window[:])
+
+        def weigh(nb, s0, n):
+            weighed = ring.tile([P, n], F32, name="weighed", tag="weighed", bufs=3, align_bytes=64)
+            nc.gpsimd.tensor_tensor(weighed[:], y_sb[nb][:, s0 : s0 + n], wgo_t[:, s0 : s0 + n], MULT)
+            return weighed
 
         y_sb = [keep.tile([P, S], F32, name="y_sb%d" % nb, align_bytes=64) for nb in range(4)]
         y_tiles = {}
@@ -266,14 +265,15 @@ def tile_list_accepted_swiglu_cache_kernel(
                     if g == 2 and i == 1:
                         down(0, c)
                         if c > 0:
-                            weigh(0, c)
+                            evacuate(0, c)
                 pending = (i, h_bf[i], g)
         quantize_h(*pending)
-        weigh(0, 0)
-        scatter(0, 0, 512, y_tiles[0, 0])
+        y_held = ring.tile([P, 512], F32, name="y_held", tag="held", bufs=1, align_bytes=64)
+        nc.vector.tensor_tensor(y_held[:], y_banks[0, 0][:], wgo_t[:, 0:512], MULT)
+        scatter(0, 0, 512, y_held[:])
         for nb in range(4):
             down(1, nb)
-            weigh(1, nb)
-        scatter(0, 512, 512, y_tiles[1, 0])
+            evacuate(1, nb)
+        scatter(0, 512, 512, weigh(0, 512, 512)[:])
         for nb in range(1, 4):
-            scatter(nb, 0, S, y_sb[nb][:])
+            scatter(nb, 0, S, weigh(nb, 0, S)[:])

@@ -14,20 +14,27 @@ U8 = mybir.dt.uint8
 FP8X4 = mybir.dt.float8_e4m3fn_x4
 FP4X4 = mybir.dt.float4_e2m1fn_x4
 MULT = mybir.AluOpType.mult
+ADD = mybir.AluOpType.add
 SILU = mybir.ActivationFunctionType.Silu
 
 P = 128
 PACK = 4
 PASS = P * PACK
-BLOCKS = H // PASS
+PASSES = H // PASS
+SCALE_ROWS = 4
 HALF = 512
 CHUNK = 128
-PIECE = 512
-LIST_ROWS = 16
+CHUNKS = HALF // CHUNK
+PER_COLUMN = 16
+ROW_BLOCKS = N // P
 WINDOWS = 3
-GROUPS = ((0, 512), (512, 512))
-VECTOR_UNITS = (range(12), range(12))
-LAST_GPSIMD_UNIT = (None, 4, 8)
+ZERO_PIECE = 512
+
+H_PLACE = {(0, 0): (0, 0), (0, 1): (0, HALF), (1, 0): (1, 0), (2, 0): (1, HALF), (1, 1): (2, 0), (2, 1): (2, HALF)}
+WU_TURN = {(0, 5): 1, (1, 0): 2}
+SCALAR_SHARE = 80
+GPSIMD_SHARE = 64
+CAST_AFTER = (6, 7)
 
 
 def tile_list_accepted_swiglu_cache_kernel(
@@ -36,244 +43,258 @@ def tile_list_accepted_swiglu_cache_kernel(
     nc = tc.nc
     with ExitStack() as ctx:
         keep = ctx.enter_context(tc.tile_pool(name="keep", bufs=1))
-        ring = ctx.enter_context(tc.tile_pool(name="ring", bufs=2))
+        ring = ctx.enter_context(tc.tile_pool(name="ring", bufs=6))
         psum = ctx.enter_context(tc.psum_pool(name="psum", bufs=1))
 
-        pick = keep.tile([P, S // LIST_ROWS], U16, name="pick")
-        place = keep.tile([P, S // LIST_ROWS], U16, name="place")
-        tab_w = keep.tile([P, T], I32, name="tab_w", align_bytes=64)
-        tab_s = keep.tile([P, T // 4], I32, name="tab_s", align_bytes=64)
-        wg_w = keep.tile([P, 2 * H], U8, name="wg_w", align_bytes=64)
-        wg_s = keep.tile([P, H], U8, name="wg_s", align_bytes=64)
-        wu_bf = [
-            keep.tile([P, PASS * PACK], BF16, name="wu_bf%d" % g, tag="wu_bf%d" % g, align_bytes=64)
-            for g in range(BLOCKS)
-        ]
-        wu_w = keep.tile([P, H], U32, name="wu_w", align_bytes=64)
-        wu_s = keep.tile([P, H], U8, name="wu_s", align_bytes=64)
-        v_w = {}
-        v_s = {}
-        h_w = [keep.tile([P, BLOCKS * n], U32, name="h_w%d" % i, align_bytes=64) for i, (s0, n) in enumerate(GROUPS)]
-        h_s = [keep.tile([P, BLOCKS * n], U8, name="h_s%d" % i, align_bytes=64) for i, (s0, n) in enumerate(GROUPS)]
-        windows = [keep.tile([P, T2], F32, name="window%d" % i, align_bytes=64) for i in range(WINDOWS - 1)]
+        def sbuf(name, shape, dtype, tag=None):
+            return keep.tile([P] + shape, dtype, name=name, tag=tag or name, align_bytes=64)
 
-        warm_in = keep.tile([P, 4], F32, name="warm_in", tag="slot_a", align_bytes=64)
-        warm_out = keep.tile([P, 4], F32, name="warm_out", align_bytes=64)
-        wg_w_raw = keep.tile([P, 2 * H // 4], I32, name="wg_w_raw", tag="slot_b", align_bytes=64)
-        wg_s_raw = keep.tile([P, H // 4], I32, name="wg_s_raw", tag="slot_d", align_bytes=64)
+        def pass_cols(g):
+            return slice(g * PASS, (g + 1) * PASS)
+
+        def entries(offsets, first, count):
+            return offsets[:, first // PER_COLUMN : (first + count) // PER_COLUMN]
+
+        pick = keep.tile([P, S // PER_COLUMN], U16, name="pick")
+        place = keep.tile([P, S // PER_COLUMN], U16, name="place")
+        tab_w = sbuf("tab_w", [T], I32)
+        tab_s = sbuf("tab_s", [T // 4], I32, "after_scale_gathers")
+        wg_w_raw = [sbuf("wg_w_raw%d" % g, [2 * PASS // 4], I32, "after_wg_words%d" % g) for g in range(PASSES)]
+        wg_s_raw = sbuf("wg_s_raw", [H // 4], I32, "after_wg_scales")
+        wg_w = sbuf("wg_w", [2 * H], U8)
+        wg_s = sbuf("wg_s", [H], U8)
+        wu_s = sbuf("wu_s", [H], U8)
+        wd_s = sbuf("wd_s", [PASSES, N // 4], I32)
+        h_w = sbuf("h_w", [PASSES, S], U32)
+        h_s = sbuf("h_s", [PASSES, S], U8)
+        y_sb = [sbuf("y_sb%d" % nb, [S], F32) for nb in range(ROW_BLOCKS - 1)]
+        windows = [sbuf("window%d" % i, [T2], F32) for i in range(WINDOWS - 1)]
+        warm_in = sbuf("warm_in", [4], F32, "after_warm_up")
+        warm_out = sbuf("warm_out", [4], F32)
+        wu_raw, wu_bf, wu_w, v_w, v_s, y_ps = {}, {}, {}, {}, {}, {}
 
         nc.vector.memset(tab_s[:], 0)
         nc.vector.memset(warm_in[:], 0.0)
         nc.scalar.activation(warm_out[:], warm_in[:], SILU)
-        nc.vector.memset(windows[0][:], 0.0)
-        nc.vector.memset(windows[1][:], 0.0)
+        for window in windows:
+            nc.vector.memset(window[:], 0.0)
         nc.vector.memset(wg_s_raw[:], 0)
+        nc.vector.memset(wd_s[:], 0)
 
-        wu_first = keep.tile([P, PACK, PASS], F32, name="wu_first", tag="slot_a", align_bytes=64)
-        wu_raw = {0: wu_first[:]}
+        def load_scale_rows(dst, src):
+            for r in range(SCALE_ROWS):
+                nc.sync.dma_start(dst[r:P:32], src[r:16:SCALE_ROWS].bitcast(I32))
 
-        def load_wu(g):
-            nc.sync.dma_start(wu_raw[g], wu[:, g * PASS : (g + 1) * PASS].rearrange("(p j) c -> p j c", j=PACK))
+        def load_wu(g, tag):
+            wu_raw[g] = sbuf("wu_raw%d" % g, [PACK, PASS], F32, tag)
+            nc.sync.dma_start(wu_raw[g][:], wu[:, pass_cols(g)].rearrange("(p j) c -> p j c", j=PACK))
 
-        nc.sync.dma_start(wg_w_raw[:], wg_words[0].bitcast(I32))
+        for g in range(PASSES):
+            nc.sync.dma_start(wg_w_raw[g][:], wg_words[0, :, 2 * g * PASS : 2 * (g + 1) * PASS].bitcast(I32))
         nc.sync.dma_start(pick[:], offs)
         nc.sync.dma_start(tab_w[:], tab_words[0].rearrange("p t i -> p (t i)").bitcast(I32))
-        for q in range(4):
-            nc.sync.dma_start(tab_s[32 * q : 32 * q + 4, :], tab_scales[0, 4 * q : 4 * q + 4, :].bitcast(I32))
-        load_wu(0)
-        for q in range(4):
-            nc.sync.dma_start(wg_s_raw[32 * q : 32 * q + 4, :], wg_scales[0, 4 * q : 4 * q + 4, :].bitcast(I32))
+        load_scale_rows(tab_s, tab_scales[0])
+        load_wu(0, "after_warm_up")
+        load_scale_rows(wg_s_raw, wg_scales[0])
         nc.sync.dma_start(place[:], offs2)
 
-        def permute_wg_words(g):
-            cols = slice(g * PASS, (g + 1) * PASS)
+        def reorder_wg_words(g):
             nc.vector.tensor_copy(
-                wg_w[:].bitcast(U16)[:, cols].rearrange("p (t b i) -> p b t i", t=PACK, i=8),
-                wg_w_raw[:].bitcast(U16)[:, cols].rearrange("p (b i t) -> p b t i", t=PACK, i=8),
+                wg_w[:].bitcast(U16)[:, pass_cols(g)].rearrange("p (t b i) -> p b t i", t=PACK, i=8),
+                wg_w_raw[g][:].bitcast(U16).rearrange("p (b i t) -> p b t i", t=PACK, i=8),
             )
 
-        def permute_wg_scales(g):
-            cols = slice(g * PASS, (g + 1) * PASS)
+        def reorder_wg_scales(g):
             nc.vector.tensor_copy(
-                wg_s[:, cols].rearrange("p (t b i) -> p b t i", t=PACK, i=16),
-                wg_s_raw[:].bitcast(U8)[:, cols].rearrange("p (b i t) -> p b t i", t=PACK, i=16),
+                wg_s[:, pass_cols(g)].rearrange("p (t b i) -> p b t i", t=PACK, i=16),
+                wg_s_raw[:].bitcast(U8)[:, pass_cols(g)].rearrange("p (b i t) -> p b t i", t=PACK, i=16),
             )
 
-        def gather_words(piece, tag):
-            v_w[piece] = keep.tile([P, PIECE], U32, name="v_w%d" % piece, tag=tag, align_bytes=64)
-            entries = pick[:, piece * PIECE // LIST_ROWS : (piece + 1) * PIECE // LIST_ROWS]
-            nc.vector.tensor_copy(v_w[piece][:], tab_w[:].bitcast(U32).indirect(entries))
+        def gather_words(half, tag):
+            v_w[half] = sbuf("v_w%d" % half, [HALF], U32, tag)
+            nc.vector.tensor_copy(v_w[half][:], tab_w[:].bitcast(U32).indirect(entries(pick, half * HALF, HALF)))
 
-        def gather_scales(piece, tag):
-            v_s[piece] = keep.tile([P, PIECE], U8, name="v_s%d" % piece, tag=tag, align_bytes=64)
-            entries = pick[:, piece * PIECE // LIST_ROWS : (piece + 1) * PIECE // LIST_ROWS]
-            nc.vector.tensor_copy(v_s[piece][:], tab_s[:].bitcast(U8).indirect(entries))
+        def gather_scales(half, tag):
+            v_s[half] = sbuf("v_s%d" % half, [HALF], U8, tag)
+            nc.vector.tensor_copy(v_s[half][:], tab_s[:].bitcast(U8).indirect(entries(pick, half * HALF, HALF)))
 
-        def cast_wu(g, copy_op, ms=slice(0, P)):
-            copy_op(
-                wu_bf[g][:].rearrange("p (t m j) -> p m j t", t=PACK, j=PACK)[:, ms],
-                wu_raw[g].rearrange("p j (m t) -> p m j t", t=PACK)[:, ms],
+        def wu_views(g, order):
+            return (
+                wu_bf[g][:].rearrange("p (t m j) -> " + order, t=PACK, j=PACK),
+                wu_raw[g][:].rearrange("p j (m t) -> " + order, t=PACK),
             )
+
+        def round_wu_on_scalar(g, ms):
+            dst, src = wu_views(g, "p m j t")
+            nc.scalar.copy(dst[:, ms], src[:, ms])
+
+        def round_wu_on_vector(g, ms):
+            dst, src = wu_views(g, "p m t j")
+            nc.vector.tensor_copy(dst[:, ms], src[:, ms])
+
+        def round_wu_on_gpsimd(g, ms):
+            dst, src = wu_views(g, "p m t j")
+            nc.gpsimd.tensor_scalar(dst[:, ms], src[:, ms], 1.0, 0.0, MULT, ADD)
 
         def quantize_wu(g):
-            cols = slice(g * PASS, (g + 1) * PASS)
-            nc.vector.quantize_mx(out=wu_w[:, cols].bitcast(FP8X4), scales=wu_s[:, cols], in_=wu_bf[g][:])
+            wu_w[g] = sbuf("wu_w%d" % g, [PASS], U32, "wu_turn%d" % g)
+            nc.vector.quantize_mx(out=wu_w[g][:].bitcast(FP8X4), scales=wu_s[:, pass_cols(g)], in_=wu_bf[g][:])
 
-        def gate(g, chunk, last):
-            piece, c0 = divmod(chunk * CHUNK, PIECE)
-            tokens = slice(c0, c0 + CHUNK)
-            a_ps = psum.tile([P, PACK, CHUNK], F32, name="a_ps", tag="a_ps", bufs=3)
+        def four_products(bank, words, scales, chunk):
+            half, c = divmod(chunk, CHUNKS)
+            tokens = slice(c * CHUNK, (c + 1) * CHUNK)
             for t in range(PACK):
-                c0 = g * PASS + t * P
                 nc.tensor.matmul_mx(
-                    out=a_ps[:, t, :],
-                    lhsT=wg_w[:, 2 * c0 : 2 * (c0 + P)].bitcast(FP4X4),
-                    lhsT_scale=wg_s[:, c0 : c0 + P],
-                    rhs=v_w[piece][:, tokens].bitcast(FP8X4),
-                    rhs_scale=v_s[piece][:, tokens],
+                    out=bank[:, t, :],
+                    lhsT=words(t),
+                    lhsT_scale=scales[:, t * P : (t + 1) * P],
+                    rhs=v_w[half][:, tokens].bitcast(FP8X4),
+                    rhs_scale=v_s[half][:, tokens],
                     start=True,
                     stop=True,
                 )
-            act = ring.tile(
-                [P, CHUNK, PACK], F32, name="act", tag="held" if last else "act", bufs=1 if last else 8, align_bytes=64
+            return bank[:].rearrange("p t n -> p n t")
+
+        def gate(g, chunk, act):
+            bank = psum.tile([P, PACK, CHUNK], F32, name="a_ps", tag="a_ps", bufs=2)
+            words = wg_w[:, 2 * g * PASS : 2 * (g + 1) * PASS]
+            a = four_products(
+                bank, lambda t: words[:, 2 * t * P : 2 * (t + 1) * P].bitcast(FP4X4), wg_s[:, pass_cols(g)], chunk
             )
-            nc.scalar.activation(act[:], a_ps[:].rearrange("p t n -> p n t"), SILU)
-            return act
+            nc.scalar.activation(act, a, SILU)
 
-        def up_times_gate(g, chunk, act, h_out, on_vector, last):
-            piece, c0 = divmod(chunk * CHUNK, PIECE)
-            tokens = slice(c0, c0 + CHUNK)
-            b_ps = psum.tile([P, PACK, CHUNK], F32, name="b_ps", tag="b_ps", bufs=3)
-            for t in range(PACK):
-                c0 = g * PASS + t * P
-                nc.tensor.matmul_mx(
-                    out=b_ps[:, t, :],
-                    lhsT=wu_w[:, c0 : c0 + P].bitcast(FP8X4),
-                    lhsT_scale=wu_s[:, c0 : c0 + P],
-                    rhs=v_w[piece][:, tokens].bitcast(FP8X4),
-                    rhs_scale=v_s[piece][:, tokens],
-                    start=True,
-                    stop=True,
-                )
-            if on_vector:
-                nc.vector.tensor_tensor(h_out, b_ps[:].rearrange("p t n -> p n t"), act[:], MULT)
+        def up(g, chunk, tag, bufs):
+            bank = psum.tile([P, PACK, CHUNK], F32, name="b_ps", tag=tag, bufs=bufs)
+            return four_products(
+                bank, lambda t: wu_w[g][:, t * P : (t + 1) * P].bitcast(FP8X4), wu_s[:, pass_cols(g)], chunk
+            )
+
+        def h_columns(g, chunk):
+            first = H_PLACE[g, chunk // CHUNKS][1] + chunk % CHUNKS * CHUNK
+            return slice(first, first + CHUNK)
+
+        def cell_on_vector(g, chunk, h_bf):
+            if (g, chunk) in WU_TURN:
+                act = sbuf("act_turn%d" % g, [CHUNK, PACK], F32, "wu_turn%d" % WU_TURN[g, chunk])
             else:
-                b_sb = ring.tile(
-                    [P, CHUNK, PACK], F32, name="b_sb", tag="held" if last else "b_sb", bufs=1 if last else 8, align_bytes=64
-                )
-                nc.scalar.copy(b_sb[:], b_ps[:].rearrange("p t n -> p n t"))
-                nc.gpsimd.tensor_tensor(
-                    h_out.rearrange("p n t -> p (n t)"),
-                    b_sb[:].rearrange("p n t -> p (n t)"),
-                    act[:].rearrange("p n t -> p (n t)"),
-                    MULT,
-                )
+                act = ring.tile([P, CHUNK, PACK], F32, name="act", align_bytes=64)
+            gate(g, chunk, act[:])
+            nc.vector.tensor_tensor(h_bf[:, h_columns(g, chunk), :], up(g, chunk, "b_ps", 3), act[:], MULT)
 
-        def unit(i, u, h_bf):
-            s0, n = GROUPS[i]
-            g, c = divmod(u, n // CHUNK)
-            chunk = s0 // CHUNK + c
-            act = gate(g, chunk, (i, u) == (1, 11))
-            up_times_gate(g, chunk, act, h_bf[:, g, c * CHUNK : (c + 1) * CHUNK, :], u in VECTOR_UNITS[i], u == LAST_GPSIMD_UNIT[i])
+        def cells_on_gpsimd(cells, h_bf, tag, bank_tag, bank_bufs):
+            act = sbuf("act_" + tag, [len(cells) * CHUNK, PACK], F32)
+            b_sb = sbuf("b_" + tag, [len(cells) * CHUNK, PACK], F32, tag)
+            for i, (g, chunk) in enumerate(cells):
+                gate(g, chunk, act[:, i * CHUNK : (i + 1) * CHUNK, :])
+                nc.scalar.copy(b_sb[:, i * CHUNK : (i + 1) * CHUNK, :], up(g, chunk, bank_tag, bank_bufs))
+            cols = slice(h_columns(*cells[0]).start, h_columns(*cells[-1]).stop)
+            flat = "p n t -> p (n t)"
+            nc.gpsimd.tensor_tensor(h_bf[:, cols, :].rearrange(flat), b_sb[:].rearrange(flat), act[:].rearrange(flat), MULT)
 
-        def quantize_h(i, h_bf, g):
-            s0, n = GROUPS[i]
-            flat = h_bf[:].rearrange("p g n t -> p (g n t)")
-            for w0, w1 in ((g * n, (g + 1) * n),):
-                nc.vector.quantize_mx(
-                    out=h_w[i][:, w0:w1].bitcast(FP8X4), scales=h_s[i][:, w0:w1], in_=flat[:, PACK * w0 : PACK * w1]
-                )
+        def quantize_h(call, h_bf):
+            nc.vector.quantize_mx(
+                out=h_w[:, call, :].bitcast(FP8X4), scales=h_s[:, call, :], in_=h_bf[:].rearrange("p n t -> p (n t)")
+            )
 
-        def down(i, nb):
-            s0, n = GROUPS[i]
+        def down(nb, half):
             rows = slice(nb * P, (nb + 1) * P)
-            y_ps = psum.tile([P, n], F32, name="y_ps", tag="y_ps", bufs=2)
-            for g in range(BLOCKS):
+            y_ps[nb, half] = psum.tile([P, HALF], F32, name="y_ps", tag="y_ps", bufs=2)
+            for g in range(PASSES):
+                call, first = H_PLACE[g, half]
                 nc.tensor.matmul_mx(
-                    out=y_ps[:],
+                    out=y_ps[nb, half][:],
                     lhsT=wd_w[:, g, rows].bitcast(FP8X4),
                     lhsT_scale=wd_s[:].bitcast(U8)[:, g, rows],
-                    rhs=h_w[i][:, g * n : (g + 1) * n].bitcast(FP8X4),
-                    rhs_scale=h_s[i][:, g * n : (g + 1) * n],
+                    rhs=h_w[:, call, first : first + HALF].bitcast(FP8X4),
+                    rhs_scale=h_s[:, call, first : first + HALF],
                     start=(g == 0),
-                    stop=(g == BLOCKS - 1),
+                    stop=(g == PASSES - 1),
                 )
-            y_banks[i, nb] = y_ps
 
-        def evacuate(i, nb):
-            s0, n = GROUPS[i]
-            nc.scalar.copy(y_sb[nb][:, s0 : s0 + n], y_banks[i, nb][:])
+        def target(nb, first, count):
+            return windows[nb % WINDOWS][:].indirect(entries(place, first, count))
 
-        def scatter(nb, s0, n, values):
-            window = windows[nb % 2]
-            nc.vector.tensor_copy(window[:].indirect(place[:, s0 // LIST_ROWS : (s0 + n) // LIST_ROWS]), values)
-            if s0 + n == S:
-                nc.sync.dma_start(out[nb * P : (nb + 1) * P, :], window[:])
+        def weigh_and_scatter(nb, first, count, values):
+            nc.vector.tensor_tensor(target(nb, first, count), values, wgo_sb[:, first : first + count], MULT)
 
-        def weigh(nb, s0, n):
-            weighed = ring.tile([P, n], F32, name="weighed", tag="weighed", bufs=3, align_bytes=64)
-            nc.gpsimd.tensor_tensor(weighed[:], y_sb[nb][:, s0 : s0 + n], wgo_t[:, s0 : s0 + n], MULT)
-            return weighed
+        def store(nb):
+            nc.sync.dma_start(out[nb * P : (nb + 1) * P, :], windows[nb % WINDOWS][:])
 
-        y_sb = [keep.tile([P, S], F32, name="y_sb%d" % nb, align_bytes=64) for nb in range(4)]
-        y_tiles = {}
-        y_banks = {}
-        def h_tile(i):
-            return keep.tile([P, BLOCKS, GROUPS[i][1], PACK], BF16, name="h_bf%d" % i, align_bytes=64)
+        first_half, second_half = slice(0, HALF), slice(HALF, S)
 
         gather_words(0, "v_w0")
         gather_scales(0, "v_s0")
-        for g in range(BLOCKS):
-            permute_wg_words(g)
-        wu_rest = keep.tile([P, BLOCKS - 1, PACK, PASS], F32, name="wu_rest", tag="slot_b", align_bytes=64)
-        for g in (1, 2):
-            wu_raw[g] = wu_rest[:, g - 1]
-            load_wu(g)
-        permute_wg_scales(0)
-        cast_wu(0, nc.scalar.copy)
+        for g in range(PASSES):
+            reorder_wg_words(g)
+        load_wu(1, "after_wg_words0")
+        load_wu(2, "after_wg_words1")
+        load_scale_rows(wd_s, wd_scales.rearrange("a q n -> q a n"))
+        windows.append(sbuf("window%d" % (WINDOWS - 1), [T2], F32, "after_wg_words2"))
+        for c0 in range(0, T2, ZERO_PIECE):
+            nc.gpsimd.memset(windows[-1][:, c0 : c0 + ZERO_PIECE], 0.0)
+        reorder_wg_scales(0)
+        wu_bf[0] = sbuf("wu_bf0", [PASS * PACK], BF16, "after_wu_codes0")
+        round_wu_on_scalar(0, slice(0, SCALAR_SHARE))
+        round_wu_on_vector(0, slice(SCALAR_SHARE, P))
         quantize_wu(0)
-        wd_w = keep.tile([P, BLOCKS, N], I32, name="wd_w", tag="slot_a", align_bytes=64)
+        reorder_wg_scales(1)
+        reorder_wg_scales(2)
+        gather_words(1, "after_wg_scales")
+        gather_scales(1, "after_warm_up")
+        wd_w = sbuf("wd_w", [PASSES, N], I32, "after_scale_gathers")
         nc.sync.dma_start(wd_w[:], wd_words.rearrange("a p n i -> p a (n i)").bitcast(I32))
-        permute_wg_scales(1)
-        permute_wg_scales(2)
-        wd_s = keep.tile([P, BLOCKS, N // 4], I32, name="wd_s", tag="slot_d", align_bytes=64)
-        nc.vector.memset(wd_s[:], 0)
-        for q in range(4):
-            nc.sync.dma_start(
-                wd_s[32 * q : 32 * q + 4, :, :],
-                wd_scales[:, 4 * q : 4 * q + 4, :].rearrange("a r n -> r a n").bitcast(I32),
-            )
-        gather_words(1, "v_w1")
-        gather_scales(1, "wu_bf0")
-        h_bf = [h_tile(0), h_tile(1)]
-        pending = None
-        for g in range(BLOCKS):
-            for i in range(2):
-                for c in range(4):
-                    unit(i, 4 * g + c, h_bf[i])
-                    step = 4 * i + c
-                    if g + 1 < BLOCKS and step in (1, 3, 5, 6):
-                        part = (1, 3, 5, 6).index(step)
-                        cast_wu(g + 1, nc.scalar.copy, slice(32 * part, 32 * part + 32))
-                    if c == 0 and pending is not None:
-                        quantize_h(*pending)
-                    if g + 1 < BLOCKS and step == 6:
-                        quantize_wu(g + 1)
-                    if g == 1 and step == 6:
-                        wgo_t = keep.tile([P, S], F32, name="wgo_t", tag="slot_b", align_bytes=64)
-                        nc.sync.dma_start(wgo_t[:], wgo)
-                    if g == 2 and i == 1:
-                        down(0, c)
-                        if c > 0:
-                            evacuate(0, c)
-                pending = (i, h_bf[i], g)
-        quantize_h(*pending)
-        y_held = ring.tile([P, 512], F32, name="y_held", tag="held", bufs=1, align_bytes=64)
-        nc.vector.tensor_tensor(y_held[:], y_banks[0, 0][:], wgo_t[:, 0:512], MULT)
-        scatter(0, 0, 512, y_held[:])
-        for nb in range(4):
-            down(1, nb)
-            evacuate(1, nb)
-        scatter(0, 512, 512, weigh(0, 512, 512)[:])
-        for nb in range(1, 4):
-            scatter(nb, 0, S, weigh(nb, 0, S)[:])
+        wu_bf[1] = sbuf("wu_bf1", [PASS * PACK], BF16, "after_wu_codes0")
+        round_wu_on_gpsimd(1, slice(0, P))
+        wgo_sb = sbuf("wgo_sb", [S], F32, "after_wg_words0")
+        nc.sync.dma_start(wgo_sb[:], wgo)
+        wu_bf[2] = sbuf("wu_bf2", [PASS * PACK], BF16)
+        round_wu_on_gpsimd(2, slice(0, GPSIMD_SHARE))
+
+        h_bf0 = sbuf("h_bf0", [S, PACK], BF16)
+        h_bf1 = sbuf("h_bf1", [S, PACK], BF16, "after_first_half")
+        for chunk in range(2 * CHUNKS):
+            cell_on_vector(0, chunk, h_bf0)
+            if (0, chunk) in WU_TURN:
+                quantize_wu(1)
+            if chunk in CAST_AFTER:
+                part = (P - GPSIMD_SHARE) // len(CAST_AFTER)
+                m0 = GPSIMD_SHARE + CAST_AFTER.index(chunk) * part
+                round_wu_on_scalar(2, slice(m0, m0 + part))
+        for chunk in range(CHUNKS):
+            cell_on_vector(1, chunk, h_bf1)
+            if (1, chunk) in WU_TURN:
+                quantize_wu(2)
+        quantize_h(0, h_bf0)
+        for chunk in range(CHUNKS):
+            cell_on_vector(2, chunk, h_bf1)
+        quantize_h(1, h_bf1)
+
+        h_bf2 = sbuf("h_bf2", [S, PACK], BF16, "after_first_half")
+        cells = [(g, chunk) for g in (1, 2) for chunk in range(CHUNKS, 2 * CHUNKS)]
+        cell_on_vector(*cells[0], h_bf2)
+        cells_on_gpsimd(cells[1:3], h_bf2, "pair0", "b_ahead", 1)
+        for nb in (0, 1):
+            down(nb, 0)
+            nc.vector.tensor_tensor(y_sb[nb][:, first_half], y_ps[nb, 0][:], wgo_sb[:, first_half], MULT)
+        cells_on_gpsimd(cells[3:5], h_bf2, "pair1", "b_ps", 3)
+        cells_on_gpsimd(cells[5:7], h_bf2, "after_pair2", "b_ps", 3)
+        cells_on_gpsimd(cells[7:8], h_bf2, "after_last_cell", "b_ps", 3)
+        down(2, 0)
+        down(3, 0)
+        y_sb.append(sbuf("y_sb3", [S], F32, "after_pair2"))
+        nc.scalar.copy(y_sb[3][:, first_half], y_ps[3, 0][:])
+        for nb in (0, 1):
+            nc.vector.tensor_copy(target(nb, 0, HALF), y_sb[nb][:, first_half])
+        quantize_h(2, h_bf2)
+
+        y_held = sbuf("y_held", [HALF], F32, "after_last_cell")
+        nc.scalar.copy(y_held[:], y_ps[2, 0][:])
+        weigh_and_scatter(2, 0, HALF, y_held[:])
+        for nb in range(ROW_BLOCKS):
+            down(nb, 1)
+            nc.scalar.copy(y_sb[nb][:, second_half], y_ps[nb, 1][:])
+        for nb in range(WINDOWS):
+            weigh_and_scatter(nb, HALF, HALF, y_sb[nb][:, second_half])
+            store(nb)
+        weigh_and_scatter(WINDOWS, 0, S, y_sb[WINDOWS][:])
+        store(WINDOWS)

@@ -32,7 +32,6 @@ ZERO_PIECE = 512
 
 H_PLACE = {(0, 0): (0, 0), (0, 1): (0, HALF), (1, 0): (1, 0), (2, 0): (1, HALF), (1, 1): (2, 0), (2, 1): (2, HALF)}
 WU_TURN = {(0, 5): 1, (1, 0): 2}
-SCALAR_SHARE = 80
 GPSIMD_SHARE = 64
 CAST_AFTER = (6, 7)
 
@@ -44,6 +43,7 @@ def tile_list_accepted_swiglu_cache_kernel(
     with ExitStack() as ctx:
         keep = ctx.enter_context(tc.tile_pool(name="keep", bufs=1))
         ring = ctx.enter_context(tc.tile_pool(name="ring", bufs=6))
+        placed = ctx.enter_context(tc.tile_pool(name="placed", bufs=1))
         psum = ctx.enter_context(tc.psum_pool(name="psum", bufs=1))
 
         def sbuf(name, shape, dtype, tag=None):
@@ -58,9 +58,9 @@ def tile_list_accepted_swiglu_cache_kernel(
         pick = keep.tile([P, S // PER_COLUMN], U16, name="pick")
         place = keep.tile([P, S // PER_COLUMN], U16, name="place")
         tab_w = sbuf("tab_w", [T], I32)
-        tab_s = sbuf("tab_s", [T // 4], I32, "after_scale_gathers")
-        wg_w_raw = [sbuf("wg_w_raw%d" % g, [2 * PASS // 4], I32, "after_wg_words%d" % g) for g in range(PASSES)]
-        wg_s_raw = sbuf("wg_s_raw", [H // 4], I32, "after_wg_scales")
+        tab_s = sbuf("tab_s", [T // 4], I32)
+        wg_w_raw = sbuf("wg_w_raw", [2 * H // 4], I32, "after_wg_words")
+        wg_s_raw = sbuf("wg_s_raw", [H // 4], I32)
         wg_w = sbuf("wg_w", [2 * H], U8)
         wg_s = sbuf("wg_s", [H], U8)
         wu_s = sbuf("wu_s", [H], U8)
@@ -69,39 +69,40 @@ def tile_list_accepted_swiglu_cache_kernel(
         h_s = sbuf("h_s", [PASSES, S], U8)
         y_sb = [sbuf("y_sb%d" % nb, [S], F32) for nb in range(ROW_BLOCKS - 1)]
         windows = [sbuf("window%d" % i, [T2], F32) for i in range(WINDOWS - 1)]
-        warm_in = sbuf("warm_in", [4], F32, "after_warm_up")
-        warm_out = sbuf("warm_out", [4], F32)
-        wu_raw, wu_bf, wu_w, v_w, v_s, y_ps = {}, {}, {}, {}, {}, {}
+        wd_w = sbuf("wd_w", [PASSES, N], I32)
+        wgo_sb = sbuf("wgo_sb", [S], F32)
+        v_s = sbuf("v_s", [S], U8)
+        wu_raw, wu_bf, wu_w, v_w, y_ps = {}, {}, {}, {}, {}
 
-        nc.vector.memset(tab_s[:], 0)
-        nc.vector.memset(warm_in[:], 0.0)
-        nc.scalar.activation(warm_out[:], warm_in[:], SILU)
+        for plane in (tab_s, wg_s_raw, wd_s):
+            nc.vector.memset(plane[:], 0)
         for window in windows:
             nc.vector.memset(window[:], 0.0)
-        nc.vector.memset(wg_s_raw[:], 0)
-        nc.vector.memset(wd_s[:], 0)
 
         def load_scale_rows(dst, src):
             for r in range(SCALE_ROWS):
                 nc.sync.dma_start(dst[r:P:32], src[r:16:SCALE_ROWS].bitcast(I32))
 
-        def load_wu(g, tag):
-            wu_raw[g] = sbuf("wu_raw%d" % g, [PACK, PASS], F32, tag)
+        def load_wu(g):
+            wu_raw[g] = sbuf("wu_raw%d" % g, [PACK, PASS], F32)
             nc.sync.dma_start(wu_raw[g][:], wu[:, pass_cols(g)].rearrange("(p j) c -> p j c", j=PACK))
 
-        for g in range(PASSES):
-            nc.sync.dma_start(wg_w_raw[g][:], wg_words[0, :, 2 * g * PASS : 2 * (g + 1) * PASS].bitcast(I32))
+        nc.sync.dma_start(wg_w_raw[:], wg_words[0].bitcast(I32))
         nc.sync.dma_start(pick[:], offs)
-        nc.sync.dma_start(tab_w[:], tab_words[0].rearrange("p t i -> p (t i)").bitcast(I32))
         load_scale_rows(tab_s, tab_scales[0])
-        load_wu(0, "after_warm_up")
+        nc.sync.dma_start(tab_w[:], tab_words[0].rearrange("p t i -> p (t i)").bitcast(I32))
         load_scale_rows(wg_s_raw, wg_scales[0])
+        for g in range(PASSES):
+            load_wu(g)
+        nc.sync.dma_start(wd_w[:], wd_words.rearrange("a p n i -> p a (n i)").bitcast(I32))
+        load_scale_rows(wd_s, wd_scales.rearrange("a q n -> q a n"))
+        nc.sync.dma_start(wgo_sb[:], wgo)
         nc.sync.dma_start(place[:], offs2)
 
         def reorder_wg_words(g):
             nc.vector.tensor_copy(
                 wg_w[:].bitcast(U16)[:, pass_cols(g)].rearrange("p (t b i) -> p b t i", t=PACK, i=8),
-                wg_w_raw[g][:].bitcast(U16).rearrange("p (b i t) -> p b t i", t=PACK, i=8),
+                wg_w_raw[:].bitcast(U16)[:, pass_cols(g)].rearrange("p (b i t) -> p b t i", t=PACK, i=8),
             )
 
         def reorder_wg_scales(g):
@@ -110,13 +111,9 @@ def tile_list_accepted_swiglu_cache_kernel(
                 wg_s_raw[:].bitcast(U8)[:, pass_cols(g)].rearrange("p (b i t) -> p b t i", t=PACK, i=16),
             )
 
-        def gather_words(half, tag):
-            v_w[half] = sbuf("v_w%d" % half, [HALF], U32, tag)
+        def gather_words(half, tile):
+            v_w[half] = tile
             nc.vector.tensor_copy(v_w[half][:], tab_w[:].bitcast(U32).indirect(entries(pick, half * HALF, HALF)))
-
-        def gather_scales(half, tag):
-            v_s[half] = sbuf("v_s%d" % half, [HALF], U8, tag)
-            nc.vector.tensor_copy(v_s[half][:], tab_s[:].bitcast(U8).indirect(entries(pick, half * HALF, HALF)))
 
         def wu_views(g, order):
             return (
@@ -149,7 +146,7 @@ def tile_list_accepted_swiglu_cache_kernel(
                     lhsT=words(t),
                     lhsT_scale=scales[:, t * P : (t + 1) * P],
                     rhs=v_w[half][:, tokens].bitcast(FP8X4),
-                    rhs_scale=v_s[half][:, tokens],
+                    rhs_scale=v_s[:, chunk * CHUNK : (chunk + 1) * CHUNK],
                     start=True,
                     stop=True,
                 )
@@ -175,11 +172,11 @@ def tile_list_accepted_swiglu_cache_kernel(
 
         def cell_on_vector(g, chunk, h_bf):
             if (g, chunk) in WU_TURN:
-                act = sbuf("act_turn%d" % g, [CHUNK, PACK], F32, "wu_turn%d" % WU_TURN[g, chunk])
+                act = sbuf("act_turn%d" % g, [CHUNK, PACK], F32, "wu_turn%d" % WU_TURN[g, chunk])[:]
             else:
-                act = ring.tile([P, CHUNK, PACK], F32, name="act", align_bytes=64)
-            gate(g, chunk, act[:])
-            nc.vector.tensor_tensor(h_bf[:, h_columns(g, chunk), :], up(g, chunk, "b_ps", 3), act[:], MULT)
+                act = ring.tile([P, CHUNK, PACK], F32, name="act", align_bytes=64)[:]
+            gate(g, chunk, act)
+            nc.vector.tensor_tensor(h_bf[:, h_columns(g, chunk), :], up(g, chunk, "b_ps", 3), act, MULT)
 
         def cells_on_gpsimd(cells, h_bf, tag, bank_tag, bank_bufs):
             act = sbuf("act_" + tag, [len(cells) * CHUNK, PACK], F32)
@@ -222,31 +219,21 @@ def tile_list_accepted_swiglu_cache_kernel(
 
         first_half, second_half = slice(0, HALF), slice(HALF, S)
 
-        gather_words(0, "v_w0")
-        gather_scales(0, "v_s0")
         for g in range(PASSES):
             reorder_wg_words(g)
-        load_wu(1, "after_wg_words0")
-        load_wu(2, "after_wg_words1")
-        load_scale_rows(wd_s, wd_scales.rearrange("a q n -> q a n"))
-        windows.append(sbuf("window%d" % (WINDOWS - 1), [T2], F32, "after_wg_words2"))
+        nc.vector.tensor_copy(v_s[:], tab_s[:].bitcast(U8).indirect(pick[:]))
+        gather_words(0, sbuf("v_w0", [HALF], U32))
+        windows.append(sbuf("window%d" % (WINDOWS - 1), [T2], F32, "after_wg_words"))
         for c0 in range(0, T2, ZERO_PIECE):
             nc.gpsimd.memset(windows[-1][:, c0 : c0 + ZERO_PIECE], 0.0)
-        reorder_wg_scales(0)
-        wu_bf[0] = sbuf("wu_bf0", [PASS * PACK], BF16, "after_wu_codes0")
-        round_wu_on_scalar(0, slice(0, SCALAR_SHARE))
-        round_wu_on_vector(0, slice(SCALAR_SHARE, P))
+        for g in range(PASSES):
+            reorder_wg_scales(g)
+        wu_bf[0] = placed.tile([P, PASS * PACK], BF16, name="wu_bf0", offset=0, align_bytes=64)
+        round_wu_on_vector(0, slice(0, P))
         quantize_wu(0)
-        reorder_wg_scales(1)
-        reorder_wg_scales(2)
-        gather_words(1, "after_wg_scales")
-        gather_scales(1, "after_warm_up")
-        wd_w = sbuf("wd_w", [PASSES, N], I32, "after_scale_gathers")
-        nc.sync.dma_start(wd_w[:], wd_words.rearrange("a p n i -> p a (n i)").bitcast(I32))
-        wu_bf[1] = sbuf("wu_bf1", [PASS * PACK], BF16, "after_wu_codes0")
+        gather_words(1, placed.tile([P, HALF], U32, name="v_w1", offset=0, align_bytes=64))
+        wu_bf[1] = placed.tile([P, PASS * PACK], BF16, name="wu_bf1", offset=4 * HALF, align_bytes=64)
         round_wu_on_gpsimd(1, slice(0, P))
-        wgo_sb = sbuf("wgo_sb", [S], F32, "after_wg_words0")
-        nc.sync.dma_start(wgo_sb[:], wgo)
         wu_bf[2] = sbuf("wu_bf2", [PASS * PACK], BF16)
         round_wu_on_gpsimd(2, slice(0, GPSIMD_SHARE))
 

@@ -19,6 +19,7 @@ SILU = mybir.ActivationFunctionType.Silu
 
 P = 128
 PACK = 4
+WORD_BYTES = 4
 PASS = P * PACK
 PASSES = H // PASS
 SCALE_ROWS = 4
@@ -33,7 +34,11 @@ ZERO_PIECE = 512
 H_PLACE = {(0, 0): (0, 0), (0, 1): (0, HALF), (1, 0): (1, 0), (2, 0): (1, HALF), (1, 1): (2, 0), (2, 1): (2, HALF)}
 WU_TURN = {(0, 5): 1, (1, 0): 2}
 GPSIMD_SHARE = 64
-CAST_AFTER = (6, 7)
+SCALAR_PARTS_AFTER = (6, 7)
+SILU_AHEAD = 6
+GATE_BANKS = 2
+UP_BANKS = 3
+DOWN_BANKS = 2
 
 
 def tile_list_accepted_swiglu_cache_kernel(
@@ -42,7 +47,7 @@ def tile_list_accepted_swiglu_cache_kernel(
     nc = tc.nc
     with ExitStack() as ctx:
         keep = ctx.enter_context(tc.tile_pool(name="keep", bufs=1))
-        ring = ctx.enter_context(tc.tile_pool(name="ring", bufs=6))
+        ring = ctx.enter_context(tc.tile_pool(name="ring", bufs=SILU_AHEAD))
         placed = ctx.enter_context(tc.tile_pool(name="placed", bufs=1))
         psum = ctx.enter_context(tc.psum_pool(name="psum", bufs=1))
 
@@ -74,8 +79,8 @@ def tile_list_accepted_swiglu_cache_kernel(
         v_s = sbuf("v_s", [S], U8)
         wu_raw, wu_bf, wu_w, v_w, y_ps = {}, {}, {}, {}, {}
 
-        for plane in (tab_s, wg_s_raw, wd_s):
-            nc.vector.memset(plane[:], 0)
+        for scale_tile in (tab_s, wg_s_raw, wd_s):
+            nc.vector.memset(scale_tile[:], 0)
         for window in windows:
             nc.vector.memset(window[:], 0.0)
 
@@ -92,7 +97,11 @@ def tile_list_accepted_swiglu_cache_kernel(
         load_scale_rows(tab_s, tab_scales[0])
         nc.sync.dma_start(tab_w[:], tab_words[0].rearrange("p t i -> p (t i)").bitcast(I32))
         load_scale_rows(wg_s_raw, wg_scales[0])
-        for g in range(PASSES):
+        wu_first = [sbuf("wu_first%d" % i, [PACK, PASS // 2], F32) for i in range(2)]
+        for i, tile in enumerate(wu_first):
+            cols = slice(i * PASS // 2, (i + 1) * PASS // 2)
+            nc.sync.dma_start(tile[:], wu[:, cols].rearrange("(p j) c -> p j c", j=PACK))
+        for g in range(1, PASSES):
             load_wu(g)
         nc.sync.dma_start(wd_w[:], wd_words.rearrange("a p n i -> p a (n i)").bitcast(I32))
         load_scale_rows(wd_s, wd_scales.rearrange("a q n -> q a n"))
@@ -125,9 +134,11 @@ def tile_list_accepted_swiglu_cache_kernel(
             dst, src = wu_views(g, "p m j t")
             nc.scalar.copy(dst[:, ms], src[:, ms])
 
-        def round_wu_on_vector(g, ms):
-            dst, src = wu_views(g, "p m t j")
-            nc.vector.tensor_copy(dst[:, ms], src[:, ms])
+        def round_first_wu_on_vector():
+            dst = wu_bf[0][:].rearrange("p (t m j) -> p m t j", t=PACK, j=PACK)
+            for i, tile in enumerate(wu_first):
+                src = tile[:].rearrange("p j (m t) -> p m t j", t=PACK)
+                nc.vector.tensor_copy(dst[:, i * P // 2 : (i + 1) * P // 2], src)
 
         def round_wu_on_gpsimd(g, ms):
             dst, src = wu_views(g, "p m t j")
@@ -153,7 +164,7 @@ def tile_list_accepted_swiglu_cache_kernel(
             return bank[:].rearrange("p t n -> p n t")
 
         def gate(g, chunk, act):
-            bank = psum.tile([P, PACK, CHUNK], F32, name="a_ps", tag="a_ps", bufs=2)
+            bank = psum.tile([P, PACK, CHUNK], F32, name="a_ps", tag="a_ps", bufs=GATE_BANKS)
             words = wg_w[:, 2 * g * PASS : 2 * (g + 1) * PASS]
             a = four_products(
                 bank, lambda t: words[:, 2 * t * P : 2 * (t + 1) * P].bitcast(FP4X4), wg_s[:, pass_cols(g)], chunk
@@ -176,7 +187,7 @@ def tile_list_accepted_swiglu_cache_kernel(
             else:
                 act = ring.tile([P, CHUNK, PACK], F32, name="act", align_bytes=64)[:]
             gate(g, chunk, act)
-            nc.vector.tensor_tensor(h_bf[:, h_columns(g, chunk), :], up(g, chunk, "b_ps", 3), act, MULT)
+            nc.vector.tensor_tensor(h_bf[:, h_columns(g, chunk), :], up(g, chunk, "b_ps", UP_BANKS), act, MULT)
 
         def cells_on_gpsimd(cells, h_bf, tag, bank_tag, bank_bufs):
             act = sbuf("act_" + tag, [len(cells) * CHUNK, PACK], F32)
@@ -195,7 +206,7 @@ def tile_list_accepted_swiglu_cache_kernel(
 
         def down(nb, half):
             rows = slice(nb * P, (nb + 1) * P)
-            y_ps[nb, half] = psum.tile([P, HALF], F32, name="y_ps", tag="y_ps", bufs=2)
+            y_ps[nb, half] = psum.tile([P, HALF], F32, name="y_ps", tag="y_ps", bufs=DOWN_BANKS)
             for g in range(PASSES):
                 call, first = H_PLACE[g, half]
                 nc.tensor.matmul_mx(
@@ -229,10 +240,10 @@ def tile_list_accepted_swiglu_cache_kernel(
         for g in range(PASSES):
             reorder_wg_scales(g)
         wu_bf[0] = placed.tile([P, PASS * PACK], BF16, name="wu_bf0", offset=0, align_bytes=64)
-        round_wu_on_vector(0, slice(0, P))
+        round_first_wu_on_vector()
         quantize_wu(0)
         gather_words(1, placed.tile([P, HALF], U32, name="v_w1", offset=0, align_bytes=64))
-        wu_bf[1] = placed.tile([P, PASS * PACK], BF16, name="wu_bf1", offset=4 * HALF, align_bytes=64)
+        wu_bf[1] = placed.tile([P, PASS * PACK], BF16, name="wu_bf1", offset=WORD_BYTES * HALF, align_bytes=64)
         round_wu_on_gpsimd(1, slice(0, P))
         wu_bf[2] = sbuf("wu_bf2", [PASS * PACK], BF16)
         round_wu_on_gpsimd(2, slice(0, GPSIMD_SHARE))
@@ -243,9 +254,9 @@ def tile_list_accepted_swiglu_cache_kernel(
             cell_on_vector(0, chunk, h_bf0)
             if (0, chunk) in WU_TURN:
                 quantize_wu(1)
-            if chunk in CAST_AFTER:
-                part = (P - GPSIMD_SHARE) // len(CAST_AFTER)
-                m0 = GPSIMD_SHARE + CAST_AFTER.index(chunk) * part
+            if chunk in SCALAR_PARTS_AFTER:
+                part = (P - GPSIMD_SHARE) // len(SCALAR_PARTS_AFTER)
+                m0 = GPSIMD_SHARE + SCALAR_PARTS_AFTER.index(chunk) * part
                 round_wu_on_scalar(2, slice(m0, m0 + part))
         for chunk in range(CHUNKS):
             cell_on_vector(1, chunk, h_bf1)
@@ -263,9 +274,9 @@ def tile_list_accepted_swiglu_cache_kernel(
         for nb in (0, 1):
             down(nb, 0)
             nc.vector.tensor_tensor(y_sb[nb][:, first_half], y_ps[nb, 0][:], wgo_sb[:, first_half], MULT)
-        cells_on_gpsimd(cells[3:5], h_bf2, "pair1", "b_ps", 3)
-        cells_on_gpsimd(cells[5:7], h_bf2, "after_pair2", "b_ps", 3)
-        cells_on_gpsimd(cells[7:8], h_bf2, "after_last_cell", "b_ps", 3)
+        cells_on_gpsimd(cells[3:5], h_bf2, "pair1", "b_ps", UP_BANKS)
+        cells_on_gpsimd(cells[5:7], h_bf2, "after_pair2", "b_ps", UP_BANKS)
+        cells_on_gpsimd(cells[7:8], h_bf2, "after_last_cell", "b_ps", UP_BANKS)
         down(2, 0)
         down(3, 0)
         y_sb.append(sbuf("y_sb3", [S], F32, "after_pair2"))

@@ -163,8 +163,8 @@ def tile_list_accepted_swiglu_cache_kernel(
                 )
             return bank[:].rearrange("p t n -> p n t")
 
-        def gate(g, chunk, act):
-            bank = psum.tile([P, PACK, CHUNK], F32, name="a_ps", tag="a_ps", bufs=GATE_BANKS)
+        def gate(g, chunk, act, tag="a_ps"):
+            bank = psum.tile([P, PACK, CHUNK], F32, name="a_ps", tag=tag, bufs=GATE_BANKS)
             words = wg_w[:, 2 * g * PASS : 2 * (g + 1) * PASS]
             a = four_products(
                 bank, lambda t: words[:, 2 * t * P : 2 * (t + 1) * P].bitcast(FP4X4), wg_s[:, pass_cols(g)], chunk
@@ -186,8 +186,8 @@ def tile_list_accepted_swiglu_cache_kernel(
                 act = sbuf("act_turn%d" % g, [CHUNK, PACK], F32, "wu_turn%d" % WU_TURN[g, chunk])[:]
             else:
                 act = ring.tile([P, CHUNK, PACK], F32, name="act", align_bytes=64)[:]
-            gate(g, chunk, act)
-            nc.vector.tensor_tensor(h_bf[:, h_columns(g, chunk), :], up(g, chunk, "b_ps", UP_BANKS), act, MULT)
+            gate(g, chunk, act, ("a_ps", "y_ps")[chunk % 2])
+            nc.vector.tensor_tensor(h_bf[:, h_columns(g, chunk), :], act, up(g, chunk, "b_ps", UP_BANKS), MULT)
 
         def cells_on_gpsimd(cells, h_bf, tag, bank_tag, bank_bufs):
             act = sbuf("act_" + tag, [len(cells) * CHUNK, PACK], F32)
@@ -273,7 +273,7 @@ def tile_list_accepted_swiglu_cache_kernel(
         cells_on_gpsimd(cells[1:3], h_bf2, "pair0", "b_ahead", 1)
         for nb in (0, 1):
             down(nb, 0)
-            nc.vector.tensor_tensor(y_sb[nb][:, first_half], y_ps[nb, 0][:], wgo_sb[:, first_half], MULT)
+            nc.vector.tensor_tensor(y_sb[nb][:, first_half], wgo_sb[:, first_half], y_ps[nb, 0][:], MULT)
         cells_on_gpsimd(cells[3:5], h_bf2, "pair1", "b_ps", UP_BANKS)
         cells_on_gpsimd(cells[5:7], h_bf2, "after_pair2", "b_ps", UP_BANKS)
         cells_on_gpsimd(cells[7:8], h_bf2, "after_last_cell", "b_ps", UP_BANKS)

@@ -35,7 +35,7 @@ H_PLACE = {(0, 0): (0, 0), (0, 1): (0, HALF), (1, 0): (1, 0), (2, 0): (1, HALF),
 WU_TURN = {(0, 5): 1, (1, 0): 2}
 GPSIMD_SHARE = 64
 SCALAR_PARTS_AFTER = (6, 7)
-SILU_AHEAD = 6
+SILU_AHEAD = 9
 GATE_BANKS = 2
 UP_BANKS = 3
 DOWN_BANKS = 2
@@ -187,7 +187,7 @@ def tile_list_accepted_swiglu_cache_kernel(
             else:
                 act = ring.tile([P, CHUNK, PACK], F32, name="act", align_bytes=64)[:]
             gate(g, chunk, act, ("a_ps", "y_ps")[chunk % 2])
-            nc.vector.tensor_tensor(h_bf[:, h_columns(g, chunk), :], act, up(g, chunk, "b_ps", UP_BANKS), MULT)
+            nc.vector.tensor_tensor(h_bf[:, h_columns(g, chunk), :], act, up(g, chunk, *(("b_ahead", 1) if g < 2 and chunk == 3 or (g, chunk) == (0, 7) else ("b_ps", UP_BANKS))), MULT)
 
         def cells_on_gpsimd(cells, h_bf, tag, bank_tag, bank_bufs):
             act = sbuf("act_" + tag, [len(cells) * CHUNK, PACK], F32)
@@ -199,9 +199,11 @@ def tile_list_accepted_swiglu_cache_kernel(
             flat = "p n t -> p (n t)"
             nc.gpsimd.tensor_tensor(h_bf[:, cols, :].rearrange(flat), b_sb[:].rearrange(flat), act[:].rearrange(flat), MULT)
 
-        def quantize_h(call, h_bf):
+        def quantize_h(call, h_bf, cols):
             nc.vector.quantize_mx(
-                out=h_w[:, call, :].bitcast(FP8X4), scales=h_s[:, call, :], in_=h_bf[:].rearrange("p n t -> p (n t)")
+                out=h_w[:, call, cols].bitcast(FP8X4),
+                scales=h_s[:, call, cols],
+                in_=h_bf[:, cols, :].rearrange("p n t -> p (n t)"),
             )
 
         def down(nb, half):
@@ -262,10 +264,11 @@ def tile_list_accepted_swiglu_cache_kernel(
             cell_on_vector(1, chunk, h_bf1)
             if (1, chunk) in WU_TURN:
                 quantize_wu(2)
-        quantize_h(0, h_bf0)
+        quantize_h(0, h_bf0, slice(0, S))
         for chunk in range(CHUNKS):
             cell_on_vector(2, chunk, h_bf1)
-        quantize_h(1, h_bf1)
+        quantize_h(1, h_bf1, first_half)
+        quantize_h(1, h_bf1, second_half)
 
         h_bf2 = sbuf("h_bf2", [S, PACK], BF16, "after_first_half")
         cells = [(g, chunk) for g in (1, 2) for chunk in range(CHUNKS, 2 * CHUNKS)]
@@ -283,7 +286,7 @@ def tile_list_accepted_swiglu_cache_kernel(
         nc.scalar.copy(y_sb[3][:, first_half], y_ps[3, 0][:])
         for nb in (0, 1):
             nc.vector.tensor_copy(target(nb, 0, HALF), y_sb[nb][:, first_half])
-        quantize_h(2, h_bf2)
+        quantize_h(2, h_bf2, slice(0, S))
 
         y_held = sbuf("y_held", [HALF], F32, "after_last_cell")
         nc.scalar.copy(y_held[:], y_ps[2, 0][:])

from contextlib import ExitStack

import concourse.mybir as mybir

K, H, N, T, S, T2 = 512, 1536, 512, 2048, 1024, 2048
FLOPS = 2 * S * (2 * K * H + H * N)

F32 = mybir.dt.float32
BF16 = mybir.dt.bfloat16
I32 = mybir.dt.int32
U32 = mybir.dt.uint32
U16 = mybir.dt.uint16
U8 = mybir.dt.uint8
FP8X4 = mybir.dt.float8_e4m3fn_x4
FP4X4 = mybir.dt.float4_e2m1fn_x4
MULT = mybir.AluOpType.mult
ADD = mybir.AluOpType.add
SILU = mybir.ActivationFunctionType.Silu

P = 128
PACK = 4
WORD_BYTES = 4
PASS = P * PACK
PASSES = H // PASS
SCALE_ROWS = 4
HALF = 512
CHUNK = 128
CHUNKS = HALF // CHUNK
PER_COLUMN = 16
ROW_BLOCKS = N // P
WINDOWS = 3
ZERO_PIECE = 512

H_PLACE = {(0, 0): (0, 0), (0, 1): (0, HALF), (1, 0): (1, 0), (2, 0): (1, HALF), (1, 1): (2, 0), (2, 1): (2, HALF)}
WU_TURN = {(0, 5): 1, (1, 0): 2}
GPSIMD_SHARE = 64
SCALAR_PARTS_AFTER = (6, 7)
SILU_AHEAD = 9
GATE_BANKS = 2
UP_BANKS = 3
DOWN_BANKS = 2


def tile_list_accepted_swiglu_cache_kernel(
    tc, tab_words, tab_scales, wg_words, wg_scales, wu, wd_words, wd_scales, wgo, offs, offs2, out
):
    nc = tc.nc
    with ExitStack() as ctx:
        keep = ctx.enter_context(tc.tile_pool(name="keep", bufs=1))
        ring = ctx.enter_context(tc.tile_pool(name="ring", bufs=SILU_AHEAD))
        placed = ctx.enter_context(tc.tile_pool(name="placed", bufs=1))
        psum = ctx.enter_context(tc.psum_pool(name="psum", bufs=1))

        def sbuf(name, shape, dtype, tag=None):
            return keep.tile([P] + shape, dtype, name=name, tag=tag or name, align_bytes=64)

        def pass_cols(g):
            return slice(g * PASS, (g + 1) * PASS)

        def entries(offsets, first, count):
            return offsets[:, first // PER_COLUMN : (first + count) // PER_COLUMN]

        pick = keep.tile([P, S // PER_COLUMN], U16, name="pick")
        place = keep.tile([P, S // PER_COLUMN], U16, name="place")
        tab_w = sbuf("tab_w", [T], I32)
        tab_s = sbuf("tab_s", [T // 4], I32)
        wg_w_raw = sbuf("wg_w_raw", [2 * H // 4], I32, "after_wg_words")
        wg_s_raw = sbuf("wg_s_raw", [H // 4], I32)
        wg_w = sbuf("wg_w", [2 * H], U8)
        wg_s = sbuf("wg_s", [H], U8)
        wu_s = sbuf("wu_s", [H], U8)
        wd_s = sbuf("wd_s", [PASSES, N // 4], I32)
        h_w = sbuf("h_w", [PASSES, S], U32)
        h_s = sbuf("h_s", [PASSES, S], U8)
        y_sb = [sbuf("y_sb%d" % nb, [S], F32) for nb in range(ROW_BLOCKS - 1)]
        windows = [sbuf("window%d" % i, [T2], F32) for i in range(WINDOWS - 1)]
        wd_w = sbuf("wd_w", [PASSES, N], I32)
        wgo_sb = sbuf("wgo_sb", [S], F32)
        v_s = sbuf("v_s", [S], U8)
        wu_raw, wu_bf, wu_w, v_w, y_ps = {}, {}, {}, {}, {}

        for scale_tile in (tab_s, wg_s_raw, wd_s):
            nc.vector.memset(scale_tile[:], 0)
        for window in windows:
            nc.vector.memset(window[:], 0.0)

        def load_scale_rows(dst, src):
            for r in range(SCALE_ROWS):
                nc.sync.dma_start(dst[r:P:32], src[r:16:SCALE_ROWS].bitcast(I32))

        def load_wu(g):
            wu_raw[g] = sbuf("wu_raw%d" % g, [PACK, PASS], F32)
            nc.sync.dma_start(wu_raw[g][:], wu[:, pass_cols(g)].rearrange("(p j) c -> p j c", j=PACK))

        nc.sync.dma_start(wg_w_raw[:], wg_words[0].bitcast(I32))
        nc.sync.dma_start(pick[:], offs)
        load_scale_rows(tab_s, tab_scales[0])
        nc.sync.dma_start(tab_w[:], tab_words[0].rearrange("p t i -> p (t i)").bitcast(I32))
        load_scale_rows(wg_s_raw, wg_scales[0])
        wu_first = [sbuf("wu_first%d" % i, [PACK, PASS // 2], F32) for i in range(2)]
        for i, tile in enumerate(wu_first):
            cols = slice(i * PASS // 2, (i + 1) * PASS // 2)
            nc.sync.dma_start(tile[:], wu[:, cols].rearrange("(p j) c -> p j c", j=PACK))
        for g in range(1, PASSES):
            load_wu(g)
        nc.sync.dma_start(wd_w[:], wd_words.rearrange("a p n i -> p a (n i)").bitcast(I32))
        load_scale_rows(wd_s, wd_scales.rearrange("a q n -> q a n"))
        nc.sync.dma_start(wgo_sb[:], wgo)
        nc.sync.dma_start(place[:], offs2)

        def reorder_wg_words(g):
            nc.vector.tensor_copy(
                wg_w[:].bitcast(U16)[:, pass_cols(g)].rearrange("p (t b i) -> p b t i", t=PACK, i=8),
                wg_w_raw[:].bitcast(U16)[:, pass_cols(g)].rearrange("p (b i t) -> p b t i", t=PACK, i=8),
            )

        def reorder_wg_scales(g):
            nc.vector.tensor_copy(
                wg_s[:, pass_cols(g)].rearrange("p (t b i) -> p b t i", t=PACK, i=16),
                wg_s_raw[:].bitcast(U8)[:, pass_cols(g)].rearrange("p (b i t) -> p b t i", t=PACK, i=16),
            )

        def gather_words(half, tile):
            v_w[half] = tile
            nc.vector.tensor_copy(v_w[half][:], tab_w[:].bitcast(U32).indirect(entries(pick, half * HALF, HALF)))

        def wu_views(g, order):
            return (
                wu_bf[g][:].rearrange("p (t m j) -> " + order, t=PACK, j=PACK),
                wu_raw[g][:].rearrange("p j (m t) -> " + order, t=PACK),
            )

        def round_wu_on_scalar(g, ms):
            dst, src = wu_views(g, "p m j t")
            nc.scalar.copy(dst[:, ms], src[:, ms])

        def round_first_wu_on_vector():
            dst = wu_bf[0][:].rearrange("p (t m j) -> p m t j", t=PACK, j=PACK)
            for i, tile in enumerate(wu_first):
                src = tile[:].rearrange("p j (m t) -> p m t j", t=PACK)
                nc.vector.tensor_copy(dst[:, i * P // 2 : (i + 1) * P // 2], src)

        def round_wu_on_gpsimd(g, ms):
            dst, src = wu_views(g, "p m t j")
            nc.gpsimd.tensor_scalar(dst[:, ms], src[:, ms], 1.0, 0.0, MULT, ADD)

        def quantize_wu(g):
            wu_w[g] = sbuf("wu_w%d" % g, [PASS], U32, "wu_turn%d" % g)
            nc.vector.quantize_mx(out=wu_w[g][:].bitcast(FP8X4), scales=wu_s[:, pass_cols(g)], in_=wu_bf[g][:])

        def four_products(bank, words, scales, chunk):
            half, c = divmod(chunk, CHUNKS)
            tokens = slice(c * CHUNK, (c + 1) * CHUNK)
            for t in range(PACK):
                nc.tensor.matmul_mx(
                    out=bank[:, t, :],
                    lhsT=words(t),
                    lhsT_scale=scales[:, t * P : (t + 1) * P],
                    rhs=v_w[half][:, tokens].bitcast(FP8X4),
                    rhs_scale=v_s[:, chunk * CHUNK : (chunk + 1) * CHUNK],
                    start=True,
                    stop=True,
                )
            return bank[:].rearrange("p t n -> p n t")

        def gate(g, chunk, act, tag="a_ps"):
            bank = psum.tile([P, PACK, CHUNK], F32, name="a_ps", tag=tag, bufs=GATE_BANKS)
            words = wg_w[:, 2 * g * PASS : 2 * (g + 1) * PASS]
            a = four_products(
                bank, lambda t: words[:, 2 * t * P : 2 * (t + 1) * P].bitcast(FP4X4), wg_s[:, pass_cols(g)], chunk
            )
            nc.scalar.activation(act, a, SILU)

        def up(g, chunk, tag, bufs):
            bank = psum.tile([P, PACK, CHUNK], F32, name="b_ps", tag=tag, bufs=bufs)
            return four_products(
                bank, lambda t: wu_w[g][:, t * P : (t + 1) * P].bitcast(FP8X4), wu_s[:, pass_cols(g)], chunk
            )

        def h_columns(g, chunk):
            first = H_PLACE[g, chunk // CHUNKS][1] + chunk % CHUNKS * CHUNK
            return slice(first, first + CHUNK)

        def cell_on_vector(g, chunk, h_bf):
            if (g, chunk) in WU_TURN:
                act = sbuf("act_turn%d" % g, [CHUNK, PACK], F32, "wu_turn%d" % WU_TURN[g, chunk])[:]
            else:
                act = ring.tile([P, CHUNK, PACK], F32, name="act", align_bytes=64)[:]
            gate(g, chunk, act, ("a_ps", "y_ps")[chunk % 2])
            nc.vector.tensor_tensor(h_bf[:, h_columns(g, chunk), :], act, up(g, chunk, *(("b_ahead", 1) if g < 2 and chunk == 3 or (g, chunk) == (0, 7) else ("b_ps", UP_BANKS))), MULT)

        def cells_on_gpsimd(cells, h_bf, tag, bank_tag, bank_bufs):
            act = sbuf("act_" + tag, [len(cells) * CHUNK, PACK], F32)
            b_sb = sbuf("b_" + tag, [len(cells) * CHUNK, PACK], F32, tag)
            for i, (g, chunk) in enumerate(cells):
                gate(g, chunk, act[:, i * CHUNK : (i + 1) * CHUNK, :])
                nc.scalar.copy(b_sb[:, i * CHUNK : (i + 1) * CHUNK, :], up(g, chunk, bank_tag, bank_bufs))
            cols = slice(h_columns(*cells[0]).start, h_columns(*cells[-1]).stop)
            flat = "p n t -> p (n t)"
            nc.gpsimd.tensor_tensor(h_bf[:, cols, :].rearrange(flat), b_sb[:].rearrange(flat), act[:].rearrange(flat), MULT)

        def quantize_h(call, h_bf, cols):
            nc.vector.quantize_mx(
                out=h_w[:, call, cols].bitcast(FP8X4),
                scales=h_s[:, call, cols],
                in_=h_bf[:, cols, :].rearrange("p n t -> p (n t)"),
            )

        def down(nb, half):
            rows = slice(nb * P, (nb + 1) * P)
            y_ps[nb, half] = psum.tile([P, HALF], F32, name="y_ps", tag="y_ps", bufs=DOWN_BANKS)
            for g in range(PASSES):
                call, first = H_PLACE[g, half]
                nc.tensor.matmul_mx(
                    out=y_ps[nb, half][:],
                    lhsT=wd_w[:, g, rows].bitcast(FP8X4),
                    lhsT_scale=wd_s[:].bitcast(U8)[:, g, rows],
                    rhs=h_w[:, call, first : first + HALF].bitcast(FP8X4),
                    rhs_scale=h_s[:, call, first : first + HALF],
                    start=(g == 0),
                    stop=(g == PASSES - 1),
                )

        def target(nb, first, count):
            return windows[nb % WINDOWS][:].indirect(entries(place, first, count))

        def weigh_and_scatter(nb, first, count, values):
            nc.vector.tensor_tensor(target(nb, first, count), values, wgo_sb[:, first : first + count], MULT)

        def store(nb):
            nc.sync.dma_start(out[nb * P : (nb + 1) * P, :], windows[nb % WINDOWS][:])

        first_half, second_half = slice(0, HALF), slice(HALF, S)

        for g in range(PASSES):
            reorder_wg_words(g)
        nc.vector.tensor_copy(v_s[:], tab_s[:].bitcast(U8).indirect(pick[:]))
        gather_words(0, sbuf("v_w0", [HALF], U32))
        windows.append(sbuf("window%d" % (WINDOWS - 1), [T2], F32, "after_wg_words"))
        for c0 in range(0, T2, ZERO_PIECE):
            nc.gpsimd.memset(windows[-1][:, c0 : c0 + ZERO_PIECE], 0.0)
        for g in range(PASSES):
            reorder_wg_scales(g)
        wu_bf[0] = placed.tile([P, PASS * PACK], BF16, name="wu_bf0", offset=0, align_bytes=64)
        round_first_wu_on_vector()
        quantize_wu(0)
        gather_words(1, placed.tile([P, HALF], U32, name="v_w1", offset=0, align_bytes=64))
        wu_bf[1] = placed.tile([P, PASS * PACK], BF16, name="wu_bf1", offset=WORD_BYTES * HALF, align_bytes=64)
        round_wu_on_gpsimd(1, slice(0, P))
        wu_bf[2] = sbuf("wu_bf2", [PASS * PACK], BF16)
        round_wu_on_gpsimd(2, slice(0, GPSIMD_SHARE))

        h_bf0 = sbuf("h_bf0", [S, PACK], BF16)
        h_bf1 = sbuf("h_bf1", [S, PACK], BF16, "after_first_half")
        for chunk in range(2 * CHUNKS):
            cell_on_vector(0, chunk, h_bf0)
            if (0, chunk) in WU_TURN:
                quantize_wu(1)
            if chunk in SCALAR_PARTS_AFTER:
                part = (P - GPSIMD_SHARE) // len(SCALAR_PARTS_AFTER)
                m0 = GPSIMD_SHARE + SCALAR_PARTS_AFTER.index(chunk) * part
                round_wu_on_scalar(2, slice(m0, m0 + part))
        for chunk in range(CHUNKS):
            cell_on_vector(1, chunk, h_bf1)
            if (1, chunk) in WU_TURN:
                quantize_wu(2)
        quantize_h(0, h_bf0, slice(0, S))
        for chunk in range(CHUNKS):
            cell_on_vector(2, chunk, h_bf1)
        quantize_h(1, h_bf1, first_half)
        quantize_h(1, h_bf1, second_half)

        h_bf2 = sbuf("h_bf2", [S, PACK], BF16, "after_first_half")
        cells = [(g, chunk) for g in (1, 2) for chunk in range(CHUNKS, 2 * CHUNKS)]
        cell_on_vector(*cells[0], h_bf2)
        cells_on_gpsimd(cells[1:3], h_bf2, "pair0", "b_ahead", 1)
        for nb in (0, 1):
            down(nb, 0)
            nc.vector.tensor_tensor(y_sb[nb][:, first_half], wgo_sb[:, first_half], y_ps[nb, 0][:], MULT)
        cells_on_gpsimd(cells[3:5], h_bf2, "pair1", "b_ps", UP_BANKS)
        cells_on_gpsimd(cells[5:7], h_bf2, "after_pair2", "b_ps", UP_BANKS)
        cells_on_gpsimd(cells[7:8], h_bf2, "after_last_cell", "b_ps", UP_BANKS)
        down(2, 0)
        down(3, 0)
        y_sb.append(sbuf("y_sb3", [S], F32, "after_pair2"))
        nc.scalar.copy(y_sb[3][:, first_half], y_ps[3, 0][:])
        for nb in (0, 1):
            nc.vector.tensor_copy(target(nb, 0, HALF), y_sb[nb][:, first_half])
        quantize_h(2, h_bf2, slice(0, S))

        y_held = sbuf("y_held", [HALF], F32, "after_last_cell")
        nc.scalar.copy(y_held[:], y_ps[2, 0][:])
        weigh_and_scatter(2, 0, HALF, y_held[:])
        for nb in range(ROW_BLOCKS):
            down(nb, 1)
            nc.scalar.copy(y_sb[nb][:, second_half], y_ps[nb, 1][:])
        for nb in range(WINDOWS):
            weigh_and_scatter(nb, HALF, HALF, y_sb[nb][:, second_half])
            store(nb)
        weigh_and_scatter(WINDOWS, 0, S, y_sb[WINDOWS][:])
        store(WINDOWS)
